import numpy as np, ml_dtypes
CORES = [23,119,17,113]
N = 4
import mx_ref
BF = ml_dtypes.bfloat16
def decode(q):
    o = []
    for b in range(4):
        e = np.zeros((128, 128, 4), np.float32); e[np.arange(128), np.arange(128), b] = 1
        o.append(mx_ref.matmul(mx_ref.quantize(e.reshape(128, 512).astype(BF)), q))
    return np.stack(o, axis=2).reshape(128, -1)
def cut(t, i, w=512):
    return t[:, w * i:w * i + w]
def f(rng, *shape):
    return mx_ref.flush((rng.standard_normal(shape, dtype=np.float32) * np.exp2(rng.integers(-2, 3, shape[:-1] + (1,)))).astype(BF))
def wide(rng, *shape, cols=0):
    v = rng.standard_normal(shape, dtype=np.float32) * np.exp2(rng.integers(-12, 13, shape)).astype(np.float32)
    if cols: v *= np.repeat(np.exp2(rng.integers(-cols, cols + 1, shape[:-2] + (1, shape[-1] // 4))) * (rng.random(shape[:-2] + (1, shape[-1] // 4)) > 0.0625), 4, axis=-1).astype(np.float32)
    return mx_ref.flush(v.astype(BF))
T, CL, O = 512, 127, 2
def taps(v):
    d = np.zeros((N, 128, 512), BF); d[:, :, :64] = mx_ref.flush(v.astype(np.float32).astype(BF)); return d
def planted(rng, a, *v):
    d = setup_inputs(rng); d["x"] = np.array(d["x"]); t = np.zeros((N, 128, 64))
    for r in range(N):
        rows = rng.permutation(512)[:len(v)]
        for m in range(len(v)):
            p, b = divmod(int(rows[m]), 4)
            d["x"][r, p, b::4] = mx_ref.flush(a[r].astype(BF)); t[r, p, b::4] = v[m][r]
    d["u"] = taps(t); return d
def setup_inputs(rng):
    return {"x": f(rng, N, 128, 4 * T), "u": taps(f(rng, N, 128, 64).astype(np.float32) * np.float32(CL * 0.005)), "w": f(rng, N, 128, 2 * O * 512)}
def setup_inputs_edge(rng):
    a = rng.uniform(-0.25, 0.25, (N, T)); a[:, :CL] = -rng.uniform(0.75, 1.25, (N, CL)); a[:, T - CL:] = rng.uniform(0.75, 1.25, (N, CL))
    return planted(rng, a, rng.uniform(0.5, 1.0, (N, 16)) * CL)
def setup_inputs_halves(rng):
    return planted(rng, rng.choice([-3.0, -1.0, 1.0, 3.0], (N, T)), rng.choice([-2.5, -1.5, -0.5, 0.5, 1.5, 2.5], (N, 16)))
def setup_inputs_last(rng):
    a = rng.choice([-1.0, 1.0], (N, T)); a[:, 0] = -1.0; a[:, T - 1] = 1.0
    return planted(rng, a, np.full((N, 16), CL + 1.0), np.full((N, 16), -1.25))
def setup_inputs_out(rng):
    return planted(rng, np.ones((N, T)), np.tile(np.repeat([-256.0, 256.0], 8), (N, 1)))
def setup_inputs_spread(rng):
    d = setup_inputs(rng); d["x"] = wide(rng, N, 128, 4 * T, cols=8)
    d["u"] = taps(f(rng, N, 128, 64).astype(np.float32) * np.float32(CL * 0.005 * 2.0 ** -10)); return d
def check_inputs(d):
    return ["u"] if (np.asarray(d["u"])[:, :, 64:].astype(np.float32) != 0).any() else []
def reference(x, u, w):
    V = np.concatenate([decode(mx_ref.quantize(x[r])) for r in range(N)], axis=1).reshape(8, 16, N * T, 4)
    y = np.zeros((N, 128, O * T), np.float32)
    for r in range(N):
        o = mx_ref.matmul(mx_ref.quantize(u[r]), mx_ref.quantize(x[r]))[:16]
        o = np.minimum(np.maximum(o, np.float32(-CL)), np.float32(CL))
        n = np.rint(o); fr = o - n
        i = np.clip(r * T + np.arange(T) + n.astype(np.int64), 0, N * T - 1); i1 = np.minimum(i + 1, N * T - 1)
        M = []
        for k in range(2):
            t = np.zeros((8, 16, T, 4), np.float32)
            for g in range(8):
                a, b = V[g][:, i[8 * k + g]], V[g][:, i1[8 * k + g]]
                t[g] = a + fr[8 * k + g][None, :, None] * (b - a)
            M.append(mx_ref.quantize(t.reshape(128, 4 * T).astype(BF)))
        for c in range(O):
            y[r][:, T * c:T * c + T] = mx_ref.matmul(mx_ref.quantize(np.ascontiguousarray(cut(w[r], c))), M[0]) + mx_ref.matmul(mx_ref.quantize(np.ascontiguousarray(cut(w[r], O + c))), M[1])
    return {"y": y}

@@ -1,0 +1,347 @@
+from concourse.bass import DstId, RemoteDMATransfer
+from concourse.mybir import dt, AluOpType, ActivationFunctionType
+
+N, TC, CL = 4, 512, 127
+HAL = 128
+OWN, RGT, LFT = 2, 514, 642
+WIN = 770
+MAGIC = 12582912.0
+
+F32, BF, U16, I32 = "float32", "bfloat16", "uint16", "int32"
+X4 = "float8_e4m3fn_x4"
+SCRATCH = {
+    "xt": ("sbuf", [128, 4 * TC + 16], BF),
+    "us": ("sbuf", [128, 16, 4], BF),
+    "zu": ("sbuf", [128, 33, 64], BF),
+    "wt": ("sbuf", [128, 4 * TC], BF),
+    "ones": ("sbuf", [128, 128], BF),
+    "unit": ("sbuf", [128, 528], BF),
+    "pidx": ("sbuf", [128, 2], I32),
+    "pint": ("sbuf", [128, 4], I32),
+    "pflt": ("sbuf", [128, 4], F32),
+    "bas0": ("sbuf", [128, 128], I32),
+    "bas": ("sbuf", [128, 128], I32),
+    "xq": ("sbuf", [128, TC], X4), "xs": ("sbuf", [128, TC], "uint8"),
+    "xq1": ("sbuf", [128, TC], X4), "xs1": ("sbuf", [128, TC], "uint8"),
+    "zq": ("sbuf", [128, 528], X4), "zs": ("sbuf", [128, 528], "uint8"),
+    "eq": ("sbuf", [128, 512], X4), "es": ("sbuf", [128, 512], "uint8"),
+    "wq": ("sbuf", [128, 512], X4), "ws": ("sbuf", [128, 512], "uint8"),
+    "hq": ("sbuf", [128, 2 * HAL], X4), "hs": ("sbuf", [128, 2 * HAL], "uint8"),
+    "vw": ("sbuf", [128, 4 * WIN], F32),
+    "dw": ("sbuf", [128, 4 * WIN], F32),
+    "yb": ("sbuf", [128, 2 * TC], F32),
+    "ps": ("psum", [128, 4096], F32),
+}
+for _k in range(2):
+    SCRATCH.update({
+        "ni%d" % _k: ("sbuf", [128, 128], I32), "pl%d" % _k: ("sbuf", [128, 128], I32),
+        "wr%d" % _k: ("sbuf", [128, 32], I32), "ab%d" % _k: ("sbuf", [128, 128], F32),
+        "sg%d" % _k: ("sbuf", [128, 128], F32), "dp%d" % _k: ("sbuf", [128, 128], I32),
+        "vl%d" % _k: ("sbuf", [128, 128], U16), "dl%d" % _k: ("sbuf", [128, 128], U16),
+        "tm%d" % _k: ("sbuf", [128, TC], F32), "rn%d" % _k: ("sbuf", [128, TC], F32),
+        "fr%d" % _k: ("sbuf", [128, 4 * TC], F32), "pp%d" % _k: ("sbuf", [128, 4 * TC], F32),
+        "mt%d" % _k: ("sbuf", [128, 4 * TC], BF),
+        "mq%d" % _k: ("sbuf", [128, TC], X4), "ms%d" % _k: ("sbuf", [128, TC], "uint8"),
+    })
+SEMAPHORES = ["cV", "cS", "cP", "cG", "sent", "arrR", "arrL", "dx1", "dx2", "du", "dwt"] + \
+    ["dy%d" % i for i in range(6)] + ["da%d" % i for i in range(4)]
+
+Op, Fn = AluOpType, ActivationFunctionType
+
+
+def scheduler(g, T):
+    queues = {"V": g.vector, "S": g.scalar, "P": g.tensor, "G": g, "Y": g.sync}
+    clock = {q: {} for q in queues}
+    done = {}
+    tick, log, scale = {}, {}, {}
+
+    def after(q, reads, writes):
+        deps = {}
+        for acc, mine in ((reads, "r"), (writes, "w")):
+            for key, lo, hi in acc:
+                for (l, h, kind, src, t, oq) in log.get(key, []):
+                    if h <= lo or hi <= l:
+                        continue
+                    bank = key[:2] == "ps"
+                    if mine == "r" and kind == "r" and not (bank and oq != q):
+                        continue
+                    if src == "c" + q and (kind == "r" or bank):
+                        continue
+                    deps[src] = max(deps.get(src, 0), t)
+        for src, t in list(deps.items()):
+            if clock[q].get(src, 0) >= t:
+                continue
+            if any(s2 != src and done[(s2, t2)].get(src, 0) >= t and clock[q].get(s2, 0) < t2 for s2, t2 in deps.items()):
+                continue
+            queues[q].wait_ge(T.sem[src], t * scale.get(src, 1))
+        for src, t in deps.items():
+            for s, v in done[(src, t)].items():
+                clock[q][s] = max(clock[q].get(s, 0), v)
+
+    def note(q, src, reads, writes):
+        tick[src] = tick.get(src, 0) + 1
+        c = dict(clock[q]) if q else {}
+        c[src] = tick[src]
+        done[(src, tick[src])] = c
+        for acc, kind in ((reads, "r"), (writes, "w")):
+            for key, lo, hi in acc:
+                log.setdefault(key, []).append((lo, hi, kind, src, tick[src], q))
+
+    def do(q, call, reads, writes):
+        after(q, reads, writes)
+        call(queues[q]).then_inc(T.sem["c" + q], 1)
+        note(q, "c" + q, reads, writes)
+
+    def dma(q, sem, out, in_, reads, writes, **kw):
+        after(q, reads, writes)
+        queues[q].dma_start(out, in_, **kw).then_inc(T.sem[sem], 16)
+        scale[sem] = 16
+        note(q, sem, reads, writes)
+
+    def arrival(sem, count, writes):
+        scale[sem] = count
+        note(None, sem, [], writes)
+
+    def drain(q):
+        for src, t in tick.items():
+            if clock[q].get(src, 0) < t:
+                queues[q].wait_ge(T.sem[src], t * scale.get(src, 1))
+
+    return do, dma, after, arrival, drain
+
+
+def rank_program(g, core, T, topo):
+    rank = T.rank_of(core)
+    if rank is None:
+        return
+    do, dma, after, arrival, drain = scheduler(g, T)
+    prev = T.cores[rank - 1] if rank > 0 else None
+    nxt = T.cores[rank + 1] if rank < N - 1 else None
+    ENG = 4
+    if nxt is not None:
+        arrival("arrR", 2 * ENG, [("hq", 0, HAL)])
+    if prev is not None:
+        arrival("arrL", 2 * ENG, [("hq", HAL, 2 * HAL)])
+
+    def quant(codes, planes, buf, c0, n, e0, lo, hi):
+        do("V", lambda v: v.quantize_mx(T[codes][:, c0:c0 + n], T[planes][:, c0:c0 + n], T[buf][:, e0:e0 + 4 * n]),
+           [(buf, lo, hi)], [(codes, c0, c0 + n)])
+
+    names = {"zq": "zs", "xq": "xs", "xq1": "xs1", "eq": "es", "wq": "ws", "hq": "hs", "mq0": "ms0", "mq1": "ms1"}
+
+    def mm(bank, n, ls, l0, rs, r0, start, stop):
+        do("P", lambda p: p.matmul_mx(T.ps[:, 512 * bank:512 * bank + n], T[ls][:, l0:l0 + 128], T[names[ls]][:, l0:l0 + 128],
+                                      T[rs][:, r0:r0 + n], T[names[rs]][:, r0:r0 + n], start, stop),
+           [(ls, l0, l0 + 128), (rs, r0, r0 + n)], [("ps%d" % bank, 0, 512)])
+
+    dma("Y", "dx1", T.xt[:, 0:1024], T.x[:, 0:1024], [], [("xt", 0, 256)])
+    dma("S", "du", T.us[:, :, :], T.u[:, 0:64], [], [("us", 0, 1)])
+    dma("Y", "dx2", T.xt[:, 1024:2048], T.x[:, 1024:2048], [], [("xt", 256, 512)])
+
+    do("G", lambda e: e.iota(T.pidx[:, 0:1], [[0, 1]], 0, 1), [], [("pidx", 0, 1)])
+    do("G", lambda e: e.iota(T.bas0[:], [[4, 128]], OWN, 0), [], [("bas0", 0, 1)])
+    do("V", lambda v: v.memset(T.ones[:], 1.0), [], [("ones", 0, 1)])
+    do("V", lambda v: v.memset(T.unit[:], 0.0), [], [("unit", 0, 1)])
+    do("G", lambda e: e.affine_select(T.unit[:, 3:515:4], T.ones[:], [[-1, 128]], Op.is_equal, 0.0, 0, 1),
+       [("ones", 0, 1)], [("unit", 0, 1)])
+    do("V", lambda v: v.memset(T.zu[:, 0:17, :], 0.0), [], [("zuz", 0, 1)])
+    do("V", lambda v: v.memset(T.xt[:, 2048:2064], 0.0), [], [("xt", 512, 516)])
+    do("V", lambda v: v.memset(T.vw[:, 0:8], 0.0), [], [("vw%d" % b, 0, 2) for b in range(4)])
+    do("V", lambda v: v.memset(T.dw[:, 0:8], 0.0), [], [("dw%d" % b, 0, 2) for b in range(4)])
+    if nxt is None:
+        for w, lo in (("dw", RGT - 1), ("vw", RGT)):
+            do("G", lambda e: e.iota(T[w][:, 4 * lo:4 * LFT], [[0, 4 * (LFT - lo)]], 0, 0, allow_small_or_imprecise_dtypes=True),
+               [], [("%s%d" % (w, b), lo, LFT) for b in range(4)])
+    do("V", lambda v: v.tensor_scalar(T.pint[:, 0:1], T.pidx[:, 0:1], 3, None, Op.bitwise_and), [("pidx", 0, 1)], [("pint", 0, 1)])
+    do("V", lambda v: v.tensor_scalar(T.pint[:, 1:2], T.pidx[:, 0:1], 2, 3, Op.arith_shift_right, Op.bitwise_and),
+       [("pidx", 0, 1)], [("pint", 1, 2)])
+    do("V", lambda v: v.tensor_copy(T.pflt[:, 0:2], T.pint[:, 0:2]), [("pint", 0, 2)], [("pflt", 0, 1)])
+    do("V", lambda v: v.tensor_scalar(T.bas[:], T.bas0[:], T.pflt[:, 1:2], None, Op.add), [("bas0", 0, 1), ("pflt", 0, 1)], [("bas", 0, 1)])
+
+    def unit_q(b):
+        quant("eq", "es", "unit", 128 * b, 128, 3 - b, 0, 1)
+
+    unit_q(0); unit_q(1)
+
+    us = [("us", 0, 1)]
+    do("V", lambda v: v.tensor_copy(T.zu[:, 0:16, 48:52], T.us[:, :, :]), us, [("zuz", 0, 1)])
+    do("V", lambda v: v.tensor_copy(T.zu[:, 0:16, 52:56], T.us[:, :, :]), us, [("zuz", 0, 1)])
+    do("S", lambda s: s.activation(T.zu[:, 17:33, 0:4], T.us[:, :, :], Fn.Copy), us, [("zuu", 0, 4)])
+    do("S", lambda s: s.activation(T.zu[:, 17:33, 4:8], T.us[:, :, :], Fn.Copy), us, [("zuu", 4, 8)])
+    do("V", lambda v: v.tensor_copy(T.zu[:, 0:16, 56:64], T.zu[:, 0:16, 48:56]), [("zuz", 0, 1)], [("zuz", 0, 1)])
+    for w in (8, 16, 32):
+        do("S", lambda s: s.activation(T.zu[:, 17:33, w:2 * w], T.zu[:, 17:33, 0:w], Fn.Copy), [("zuu", 0, w)], [("zuu", w, 2 * w)])
+    do("V", lambda v: v.quantize_mx(T.zq[:, 0:272], T.zs[:, 0:272], T.zu[:, 0:17, :]), [("zuz", 0, 1)], [("zq", 0, 272)])
+
+    quant("xq", "xs", "xt", 0, 256, 0, 0, 256)
+    quant("xq", "xs", "xt", 256, 256, 1024, 256, 512)
+    quant("xq1", "xs1", "xt", 0, 254, 4, 1, 255)
+    quant("xq1", "xs1", "xt", 254, 258, 1020, 255, 513)
+    do("V", lambda v: v.quantize_mx(T.zq[:, 272:528], T.zs[:, 272:528], T.zu[:, 17:33, :]), [("zuu", 0, 64)], [("zq", 272, 528)])
+
+    sends = []
+    if prev is not None:
+        sends.append((prev, 0, 0, "arrR"))
+    if nxt is not None:
+        sends.append((nxt, TC - HAL, HAL, "arrL"))
+    after("G", [("xq", c0, c0 + HAL) for _, c0, _, _ in sends], [])
+    for plane in (0, 1):
+        tr = []
+        for i, (dst, c0, d0, sem) in enumerate(sends):
+            rid, pid, _ = topo.addr(dst)
+            eng = topo.engines(core, dst)[ENG * i:ENG * i + ENG]
+            s, d = (T.xs[:, c0:c0 + HAL], T.hs[:, d0:d0 + HAL]) if plane else \
+                (T.xq[:, c0:c0 + HAL].bitcast(dt.uint8), T.hq[:, d0:d0 + HAL].bitcast(dt.uint8))
+            tr.append(RemoteDMATransfer(dst_ids=[DstId(rid=rid, pnc=pid)], dma_engine_mask=sum(1 << e for e in eng),
+                                        remote_sem=T.sem[sem], src=s, dst=d))
+        g.remote_dma_fused(tr, local_sem=T.sem.sent)
+    sent = 2 * ENG * len(sends)
+
+    after("Y", [("xt", 0, 512)], [])
+    dma("Y", "dwt", T.wt[:], T.w[:], [], [("wt", 0, 1)])
+
+    def unpack_mm(b):
+        mm(b, TC, "eq", 128 * b, "xq", 0, True, True)
+
+    def unpack_copy(b):
+        do("S", lambda s: s.activation(T.vw[:, 4 * OWN + b:4 * RGT:4], T.ps[:, 512 * b:512 * b + 512], Fn.Copy),
+           [("ps%d" % b, 0, 512)], [("vw%d" % b, OWN, RGT)])
+
+    def diff(b):
+        do("V", lambda v: v.tensor_tensor(T.dw[:, 4 * OWN + b:4 * (RGT - 1):4], T.ps[:, 512 * b + 1:512 * b + 512],
+                                          T.vw[:, 4 * OWN + b:4 * (RGT - 1):4], Op.subtract),
+           [("ps%d" % b, 0, 512), ("vw%d" % b, OWN, RGT - 1)], [("dw%d" % b, OWN, RGT - 1)])
+
+    def offs_mm(k):
+        mm(6 + k, TC, "zq", 272 + 128 * k, "xq", 0, True, True)
+
+    def list_mm(k):
+        for n, a in enumerate((0, 2, 1, 3)):
+            mm(4 + k, 510, "zq", 128 * k + 12 - 4 * a, "xq1" if a % 2 else "xq", a - a % 2, n == 0, n == 3)
+
+    def frac_n(k, j0, j1):
+        do("S", lambda s: s.activation(T["tm%d" % k][:, j0:j1], T.ps[:, 512 * (6 + k) + j0:512 * (6 + k) + j1], Fn.Copy, bias=MAGIC),
+           [("ps%d" % (6 + k), 0, 512)], [("tm%d" % k, j0, j1)])
+        do("S", lambda s: s.activation(T["rn%d" % k][:, j0:j1], T["tm%d" % k][:, j0:j1], Fn.Copy, bias=-MAGIC),
+           [("tm%d" % k, j0, j1)], [("rn%d" % k, j0, j1)])
+
+    def frac_sub(k, j0, j1):
+        do("V", lambda v: v.tensor_tensor(T["fr%d" % k][:, 4 * j0:4 * j1:4], T.ps[:, 512 * (6 + k) + j0:512 * (6 + k) + j1],
+                                          T["rn%d" % k][:, j0:j1], Op.subtract),
+           [("ps%d" % (6 + k), 0, 512), ("rn%d" % k, j0, j1)], [("fr%d0" % k, j0, j1)])
+
+    def frac_rep(q, k, j0, j1, bs):
+        for b in bs:
+            out, in_ = T["fr%d" % k][:, 4 * j0 + b:4 * j1:4], T["fr%d" % k][:, 4 * j0:4 * j1:4]
+            call = {"S": lambda s: s.activation(out, in_, Fn.Copy), "V": lambda v: v.tensor_copy(out, in_),
+                    "G": lambda e: e.affine_select(out, in_, [[1, j1 - j0]], Op.is_gt, 0.0, 1, 0)}[q]
+            do(q, call, [("fr%d0" % k, j0, j1)], [("fr%d%d" % (k, b), j0, j1)])
+
+    def inside(k):
+        ab, sg = T["ab%d" % k], T["sg%d" % k]
+        do("S", lambda s: s.activation(ab[:], T.ps[:, 512 * (4 + k):512 * (4 + k) + 509:4], Fn.Abs), [("ps%d" % (4 + k), 0, 512)], [("ab%d" % k, 0, 128)])
+        do("S", lambda s: s.activation(sg[:], ab[:], Fn.Sign, bias=float(CL), scale=-1.0), [("ab%d" % k, 0, 128)], [("sg%d" % k, 0, 128)])
+
+    def lists(k):
+        ni, pl, wr, sg, dp, vl, dl = (T[n + str(k)] for n in ("ni", "pl", "wr", "sg", "dp", "vl", "dl"))
+        key = lambda n, lo=0, hi=128: (n + str(k), lo, hi)
+        d = T.ps[:, 512 * (4 + k):512 * (4 + k) + 509:4]
+        do("V", lambda v: v.tensor_scalar(ni[:], d, float(-CL), float(CL), Op.max, Op.min), [("ps%d" % (4 + k), 0, 512)], [key("ni")])
+        do("V", lambda v: v.tensor_tensor(pl[:], ni[:], T.bas[:], Op.add), [key("ni"), ("bas", 0, 1)], [key("pl")])
+        if prev is None:
+            do("V", lambda v: v.tensor_scalar(pl[:, 0:32], pl[:, 0:32], float(OWN), None, Op.max), [key("pl", 0, 32)], [key("pl", 0, 32)])
+        else:
+            do("V", lambda v: v.tensor_scalar(wr[:], pl[:, 0:32], float(OWN), float(WIN - OWN), Op.is_lt, Op.mult), [key("pl", 0, 32)], [key("wr")])
+            do("V", lambda v: v.tensor_tensor(pl[:, 0:32], pl[:, 0:32], wr[:], Op.add), [key("pl", 0, 32), key("wr")], [key("pl", 0, 32)])
+        if nxt is None:
+            do("V", lambda v: v.tensor_scalar(pl[:, 96:128], pl[:, 96:128], float(RGT - 1), None, Op.min), [key("pl", 96, 128)], [key("pl", 96, 128)])
+        do("V", lambda v: v.tensor_scalar(vl[:], pl[:], 4.0, T.pflt[:, 0:1], Op.mult, Op.add), [key("pl"), ("pflt", 0, 1)], [key("vl")])
+        do("V", lambda v: v.tensor_tensor(dp[:], pl[:], sg[:], Op.mult), [key("pl"), key("sg")], [key("dp")])
+        do("V", lambda v: v.tensor_scalar(dl[:], dp[:], 4.0, T.pflt[:, 0:1], Op.mult, Op.add), [key("dp"), ("pflt", 0, 1)], [key("dl")])
+
+    def slope(k, j0, j1, end):
+        do("V", lambda v: v.tensor_tensor(T["pp%d" % k][:, 4 * j0:4 * j1], T.dw[:, 0:4 * end].indirect(T["dl%d" % k][:, j0 // 4:j1 // 4]),
+                                          T["fr%d" % k][:, 4 * j0:4 * j1], Op.mult),
+           [("dw%d" % b, 0, end) for b in range(4)] + [("fr%d%d" % (k, b), j0, j1) for b in range(4)] + [("dl%d" % k, 0, 128)],
+           [("pp%d" % k, j0, j1)])
+
+    def tap(k, j0, j1, end):
+        do("V", lambda v: v.tensor_tensor(T["mt%d" % k][:, 4 * j0:4 * j1], T.vw[:, 0:4 * end].indirect(T["vl%d" % k][:, j0 // 4:j1 // 4]),
+                                          T["pp%d" % k][:, 4 * j0:4 * j1], Op.add),
+           [("vw%d" % b, 0, end) for b in range(4)] + [("pp%d" % k, j0, j1), ("vl%d" % k, 0, 128)], [("mt%d" % k, j0, j1)])
+
+    def far_v(k, j0, j1, end):
+        do("S", lambda s: s.activation(T["mt%d" % k][:, 4 * j0:4 * j1], T.vw[:, 0:4 * end].indirect(T["vl%d" % k][:, j0 // 4:j1 // 4]), Fn.Copy),
+           [("vw%d" % b, 0, end) for b in range(4)] + [("vl%d" % k, 0, 128)], [("mt%d" % k, j0, j1)])
+
+    def far_add(k, j0, j1, sem):
+        dma("G", sem, T["mt%d" % k][:, 4 * j0:4 * j1], T["pp%d" % k][:, 4 * j0:4 * j1],
+            [("pp%d" % k, j0, j1), ("mt%d" % k, j0, j1)], [("mt%d" % k, j0, j1)], accum_op=Op.add)
+
+    def finish(j0, j1, banks, n, first=0, last=False):
+        for k in (first, 1 - first):
+            quant("mq%d" % k, "ms%d" % k, "mt%d" % k, j0, j1 - j0, 4 * j0, j0, j1)
+            for o in range(2):
+                mm(banks[o], j1 - j0, "wq", 128 * (2 * k + o), "mq%d" % k, j0, k == first, k != first)
+        for o in range(2):
+            src, dst = T.ps[:, 512 * banks[o]:512 * banks[o] + j1 - j0], T.yb[:, TC * o + j0:TC * o + j1]
+            acc = ([("ps%d" % banks[o], 0, 512)], [("yb%d" % o, j0, j1)])
+            if last and o == 1:
+                do("V", lambda v: v.tensor_copy(dst, src), *acc)
+            else:
+                do("S", lambda s: s.activation(dst, src, Fn.Copy), *acc)
+            dma("S" if last and o == 1 else "Y", "dy%d" % (2 * n + o), T.y[:, TC * o + j0:TC * o + j1], dst, [("yb%d" % o, j0, j1)], [])
+
+    A, LO, HI = (128, 384), (0, 128), (384, 512)
+    unpack_mm(0); unpack_mm(1); offs_mm(0); list_mm(0)
+    unpack_copy(0); unpack_copy(1)
+    frac_n(0, *A); frac_n(0, *LO); frac_n(0, *HI)
+    diff(0); diff(1); frac_sub(0, *A); frac_rep("S", 0, *A, (1, 2)); frac_rep("V", 0, *A, (3,))
+    unit_q(2); unit_q(3)
+    unpack_mm(2); unpack_mm(3); offs_mm(1); list_mm(1)
+    frac_sub(0, *LO); frac_sub(0, *HI); frac_rep("G", 0, *LO, (2, 3)); frac_rep("G", 0, *HI, (2, 3))
+    inside(0); unpack_copy(2); unpack_copy(3); lists(0)
+    diff(2); diff(3)
+    frac_n(1, 0, TC)
+    slope(0, *A, RGT - 1)
+    far_v(0, *A, RGT)
+    frac_sub(1, 0, TC)
+    inside(1)
+    frac_rep("G", 1, *A, (3,)); frac_rep("S", 1, *A, (1, 2))
+    far_add(0, *A, "da0")
+    frac_rep("G", 1, *LO, (3,)); frac_rep("G", 1, *HI, (3,))
+    lists(1)
+    slope(1, *A, RGT - 1)
+    far_v(1, *A, RGT); far_add(1, *A, "da1")
+
+    h0, h1 = (0 if nxt is not None else HAL), (2 * HAL if prev is not None else HAL)
+    w0, w1 = RGT + h0, RGT + h1
+    e = 1 if nxt is None else 0
+    for b in range(4):
+        mm(b, h1 - h0, "eq", 128 * b, "hq", h0, True, True)
+    for b in range(4):
+        do("S", lambda s: s.activation(T.vw[:, 4 * w0 + b:4 * w1:4], T.ps[:, 512 * b:512 * b + w1 - w0], Fn.Copy),
+           [("ps%d" % b, 0, 512)], [("vw%d" % b, w0, w1)])
+        do("V", lambda v: v.tensor_tensor(T.dw[:, 4 * (w0 - 1 + e) + b:4 * (w1 - 1):4], T.ps[:, 512 * b + e:512 * b + w1 - w0],
+                                          T.vw[:, 4 * (w0 - 1 + e) + b:4 * (w1 - 1):4], Op.subtract),
+           [("ps%d" % b, 0, 512), ("vw%d" % b, w0 - 1 + e, w1 - 1)], [("dw%d" % b, w0 - 1 + e, w1 - 1)])
+    if prev is not None:
+        do("V", lambda v: v.tensor_tensor(T.dw[:, 4 * (WIN - 1):4 * WIN], T.vw[:, 4 * OWN:4 * OWN + 4], T.vw[:, 4 * (WIN - 1):4 * WIN], Op.subtract),
+           [("vw%d" % b, OWN, OWN + 1) for b in range(4)] + [("vw%d" % b, WIN - 1, WIN) for b in range(4)],
+           [("dw%d" % b, WIN - 1, WIN) for b in range(4)])
+    frac_rep("S", 0, *LO, (1,)); frac_rep("S", 0, *HI, (1,)); frac_rep("S", 1, *LO, (1, 2)); frac_rep("S", 1, *HI, (1, 2))
+
+    L = LO + ((RGT - 1, RGT) if prev is None else (WIN, WIN))
+    R = HI + ((LFT - 1, LFT) if nxt is not None else (RGT, RGT))
+    E1, E2 = (L, R) if prev is None else (R, L)
+    slope(0, *E1[:3]); far_v(0, *E1[:2], E1[3]); far_add(0, *E1[:2], "da2")
+    slope(0, *E2[:3]); far_v(0, *E2[:2], E2[3]); far_add(0, *E2[:2], "da3")
+    slope(1, *E1[:3]); slope(1, *E2[:3])
+    tap(1, *E1[:2], E1[3])
+    quant("wq", "ws", "wt", 0, 512, 0, 0, 1)
+    finish(*A, (4, 5), 0)
+    finish(*E1[:2], (6, 7), 1)
+    tap(1, *E2[:2], E2[3])
+    finish(*E2[:2], (0, 1), 2, first=1, last=True)
+    g.wait_ge(T.sem.sent, sent)
+    drain("Y")

@@ -3,48 +3,42 @@ from concourse.mybir import dt, AluOpType, ActivationFunctionType
 
 N, TC, CL = 4, 512, 127
 HAL = 128
-OWN, RGT, LFT = 2, 514, 642
-WIN = 770
+OWN, RGT, WIN = 128, 640, 768
 MAGIC = 12582912.0
+A, E = 0, 1
+RUNS = ((128, 256), (0, 384))
 
 F32, BF, U16, I32 = "float32", "bfloat16", "uint16", "int32"
 X4 = "float8_e4m3fn_x4"
 SCRATCH = {
-    "xt": ("sbuf", [128, 4 * TC + 16], BF),
+    "xt": ("sbuf", [128, 4 * TC], BF),
     "us": ("sbuf", [128, 16, 4], BF),
-    "zu": ("sbuf", [128, 33, 64], BF),
+    "zo": ("sbuf", [128, 16, 64], BF),
+    "zl": ("sbuf", [128, 9, 64], BF),
     "wt": ("sbuf", [128, 4 * TC], BF),
     "ones": ("sbuf", [128, 128], BF),
     "unit": ("sbuf", [128, 528], BF),
     "pidx": ("sbuf", [128, 2], I32),
     "pint": ("sbuf", [128, 4], I32),
     "pflt": ("sbuf", [128, 4], F32),
-    "bas0": ("sbuf", [128, 128], I32),
-    "bas": ("sbuf", [128, 128], I32),
+    "bas0": ("sbuf", [128, 128], F32),
     "xq": ("sbuf", [128, TC], X4), "xs": ("sbuf", [128, TC], "uint8"),
-    "xq1": ("sbuf", [128, TC], X4), "xs1": ("sbuf", [128, TC], "uint8"),
-    "zq": ("sbuf", [128, 528], X4), "zs": ("sbuf", [128, 528], "uint8"),
+    "zq": ("sbuf", [128, 400], X4), "zs": ("sbuf", [128, 400], "uint8"),
     "eq": ("sbuf", [128, 512], X4), "es": ("sbuf", [128, 512], "uint8"),
     "wq": ("sbuf", [128, 512], X4), "ws": ("sbuf", [128, 512], "uint8"),
     "hq": ("sbuf", [128, 2 * HAL], X4), "hs": ("sbuf", [128, 2 * HAL], "uint8"),
-    "vw": ("sbuf", [128, 4 * WIN], F32),
-    "dw": ("sbuf", [128, 4 * WIN], F32),
+    "mq": ("sbuf", [128, 2 * TC], X4), "ms": ("sbuf", [128, 2 * TC], "uint8"),
+    "vw": ("sbuf", [128, 4 * WIN], F32), "dw": ("sbuf", [128, 4 * WIN], F32),
+    "tm": ("sbuf", [128, 2 * TC], F32), "rn": ("sbuf", [128, 2 * TC], F32),
+    "fr": ("sbuf", [128, 8 * TC], F32), "pp": ("sbuf", [128, 8 * TC], F32), "mt": ("sbuf", [128, 8 * TC], BF),
+    "bas": ("sbuf", [128, 256], F32), "ni": ("sbuf", [128, 256], I32), "pl": ("sbuf", [128, 256], I32),
+    "dp": ("sbuf", [128, 256], I32), "ab": ("sbuf", [128, 256], F32), "sg": ("sbuf", [128, 256], F32),
+    "vl": ("sbuf", [128, 256], U16), "dl": ("sbuf", [128, 256], U16),
     "yb": ("sbuf", [128, 2 * TC], F32),
     "ps": ("psum", [128, 4096], F32),
 }
-for _k in range(2):
-    SCRATCH.update({
-        "ni%d" % _k: ("sbuf", [128, 128], I32), "pl%d" % _k: ("sbuf", [128, 128], I32),
-        "wr%d" % _k: ("sbuf", [128, 32], I32), "ab%d" % _k: ("sbuf", [128, 128], F32),
-        "sg%d" % _k: ("sbuf", [128, 128], F32), "dp%d" % _k: ("sbuf", [128, 128], I32),
-        "vl%d" % _k: ("sbuf", [128, 128], U16), "dl%d" % _k: ("sbuf", [128, 128], U16),
-        "tm%d" % _k: ("sbuf", [128, TC], F32), "rn%d" % _k: ("sbuf", [128, TC], F32),
-        "fr%d" % _k: ("sbuf", [128, 4 * TC], F32), "pp%d" % _k: ("sbuf", [128, 4 * TC], F32),
-        "mt%d" % _k: ("sbuf", [128, 4 * TC], BF),
-        "mq%d" % _k: ("sbuf", [128, TC], X4), "ms%d" % _k: ("sbuf", [128, TC], "uint8"),
-    })
 SEMAPHORES = ["cV", "cS", "cP", "cG", "sent", "arrR", "arrL", "dx1", "dx2", "du", "dwt"] + \
-    ["dy%d" % i for i in range(6)] + ["da%d" % i for i in range(4)]
+    ["dy%d" % i for i in range(12)] + ["da%d" % i for i in range(6)]
 
 Op, Fn = AluOpType, ActivationFunctionType
 
@@ -118,230 +112,297 @@ def rank_program(g, core, T, topo):
     prev = T.cores[rank - 1] if rank > 0 else None
     nxt = T.cores[rank + 1] if rank < N - 1 else None
     ENG = 4
-    if nxt is not None:
-        arrival("arrR", 2 * ENG, [("hq", 0, HAL)])
     if prev is not None:
-        arrival("arrL", 2 * ENG, [("hq", HAL, 2 * HAL)])
+        arrival("arrL", 2 * ENG, [("hq", 0, HAL)])
+    if nxt is not None:
+        arrival("arrR", 2 * ENG, [("hq", HAL, 2 * HAL)])
+    first = (OWN, 0 if prev is not None else OWN - 2)
+    end = (RGT, WIN if nxt is not None else RGT)
+    each = lambda name, lo, hi, bs=range(4): [("%s%d" % (name, b), lo, hi) for b in bs]
+    bank = lambda n: [("ps%d" % n, 0, 512)]
 
     def quant(codes, planes, buf, c0, n, e0, lo, hi):
         do("V", lambda v: v.quantize_mx(T[codes][:, c0:c0 + n], T[planes][:, c0:c0 + n], T[buf][:, e0:e0 + 4 * n]),
            [(buf, lo, hi)], [(codes, c0, c0 + n)])
 
-    names = {"zq": "zs", "xq": "xs", "xq1": "xs1", "eq": "es", "wq": "ws", "hq": "hs", "mq0": "ms0", "mq1": "ms1"}
+    names = {"zq": "zs", "xq": "xs", "eq": "es", "wq": "ws", "hq": "hs", "mq": "ms"}
 
-    def mm(bank, n, ls, l0, rs, r0, start, stop):
-        do("P", lambda p: p.matmul_mx(T.ps[:, 512 * bank:512 * bank + n], T[ls][:, l0:l0 + 128], T[names[ls]][:, l0:l0 + 128],
-                                      T[rs][:, r0:r0 + n], T[names[rs]][:, r0:r0 + n], start, stop),
-           [(ls, l0, l0 + 128), (rs, r0, r0 + n)], [("ps%d" % bank, 0, 512)])
+    def mm(n, cols, ls, l0, rs, r0, start, stop):
+        do("P", lambda p: p.matmul_mx(T.ps[:, 512 * n:512 * n + cols], T[ls][:, l0:l0 + 128], T[names[ls]][:, l0:l0 + 128],
+                                      T[rs][:, r0:r0 + cols], T[names[rs]][:, r0:r0 + cols], start, stop),
+           [(ls, l0, l0 + 128), (rs, r0, r0 + cols)], bank(n))
+
+    def copy(q, out, in_, reads, writes):
+        if q == "G":
+            do(q, lambda e: e.affine_select(out, in_, [[1, out.shape[1]]], Op.is_gt, 0.0, 1, 0), reads, writes)
+        else:
+            do(q, lambda e: e.activation(out, in_, Fn.Copy) if q == "S" else e.tensor_copy(out, in_), reads, writes)
 
     dma("Y", "dx1", T.xt[:, 0:1024], T.x[:, 0:1024], [], [("xt", 0, 256)])
     dma("S", "du", T.us[:, :, :], T.u[:, 0:64], [], [("us", 0, 1)])
     dma("Y", "dx2", T.xt[:, 1024:2048], T.x[:, 1024:2048], [], [("xt", 256, 512)])
 
     do("G", lambda e: e.iota(T.pidx[:, 0:1], [[0, 1]], 0, 1), [], [("pidx", 0, 1)])
-    do("G", lambda e: e.iota(T.bas0[:], [[4, 128]], OWN, 0), [], [("bas0", 0, 1)])
     do("V", lambda v: v.memset(T.ones[:], 1.0), [], [("ones", 0, 1)])
     do("V", lambda v: v.memset(T.unit[:], 0.0), [], [("unit", 0, 1)])
     do("G", lambda e: e.affine_select(T.unit[:, 3:515:4], T.ones[:], [[-1, 128]], Op.is_equal, 0.0, 0, 1),
        [("ones", 0, 1)], [("unit", 0, 1)])
-    do("V", lambda v: v.memset(T.zu[:, 0:17, :], 0.0), [], [("zuz", 0, 1)])
-    do("V", lambda v: v.memset(T.xt[:, 2048:2064], 0.0), [], [("xt", 512, 516)])
-    do("V", lambda v: v.memset(T.vw[:, 0:8], 0.0), [], [("vw%d" % b, 0, 2) for b in range(4)])
-    do("V", lambda v: v.memset(T.dw[:, 0:8], 0.0), [], [("dw%d" % b, 0, 2) for b in range(4)])
+    do("V", lambda v: v.memset(T.zl[:, :, :], 0.0), [], [("zl", 0, 2)])
+    whole_numbers = lambda out, step: lambda e: e.iota(out, [[step, out.shape[1]]], 0, 0, allow_small_or_imprecise_dtypes=True)
+    do("G", whole_numbers(T.bas0[:], 1), [], [("bas0", 0, 1)])
+    zeros = [("dw", OWN, OWN + 1), ("dw", first[E], first[E] + 1)]
+    if prev is None:
+        zeros = [("dw", OWN - 2, OWN + 1), ("vw", OWN - 2, OWN)]
     if nxt is None:
-        for w, lo in (("dw", RGT - 1), ("vw", RGT)):
-            do("G", lambda e: e.iota(T[w][:, 4 * lo:4 * LFT], [[0, 4 * (LFT - lo)]], 0, 0, allow_small_or_imprecise_dtypes=True),
-               [], [("%s%d" % (w, b), lo, LFT) for b in range(4)])
+        zeros.append(("dw", RGT - 1, RGT))
+    for w, lo, hi in zeros:
+        do("G", whole_numbers(T[w][:, 4 * lo:4 * hi], 0), [], each(w, lo, hi))
     do("V", lambda v: v.tensor_scalar(T.pint[:, 0:1], T.pidx[:, 0:1], 3, None, Op.bitwise_and), [("pidx", 0, 1)], [("pint", 0, 1)])
-    do("V", lambda v: v.tensor_scalar(T.pint[:, 1:2], T.pidx[:, 0:1], 2, 3, Op.arith_shift_right, Op.bitwise_and),
+    do("V", lambda v: v.tensor_scalar(T.pint[:, 1:2], T.pidx[:, 0:1], 2, 1, Op.arith_shift_right, Op.bitwise_and),
        [("pidx", 0, 1)], [("pint", 1, 2)])
-    do("V", lambda v: v.tensor_copy(T.pflt[:, 0:2], T.pint[:, 0:2]), [("pint", 0, 2)], [("pflt", 0, 1)])
-    do("V", lambda v: v.tensor_scalar(T.bas[:], T.bas0[:], T.pflt[:, 1:2], None, Op.add), [("bas0", 0, 1), ("pflt", 0, 1)], [("bas", 0, 1)])
 
-    def unit_q(b):
+    def quant_e(b):
         quant("eq", "es", "unit", 128 * b, 128, 3 - b, 0, 1)
 
-    unit_q(0); unit_q(1)
+    quant_e(0)
+    do("V", lambda v: v.tensor_copy(T.pflt[:, 0:2], T.pint[:, 0:2]), [("pint", 0, 2)], [("pflt", 0, 1)])
+    for s in (A, E):
+        do("S", lambda e: e.activation(T.pflt[:, 2 + s:3 + s], T.pflt[:, 1:2], Fn.Copy, bias=float(OWN + RUNS[s][0] - first[s]),
+                                       scale=float(RUNS[s][1] - RUNS[s][0])), [("pflt", 0, 1)], [("pflt", 2 + s, 3 + s)])
 
-    us = [("us", 0, 1)]
-    do("V", lambda v: v.tensor_copy(T.zu[:, 0:16, 48:52], T.us[:, :, :]), us, [("zuz", 0, 1)])
-    do("V", lambda v: v.tensor_copy(T.zu[:, 0:16, 52:56], T.us[:, :, :]), us, [("zuz", 0, 1)])
-    do("S", lambda s: s.activation(T.zu[:, 17:33, 0:4], T.us[:, :, :], Fn.Copy), us, [("zuu", 0, 4)])
-    do("S", lambda s: s.activation(T.zu[:, 17:33, 4:8], T.us[:, :, :], Fn.Copy), us, [("zuu", 4, 8)])
-    do("V", lambda v: v.tensor_copy(T.zu[:, 0:16, 56:64], T.zu[:, 0:16, 48:56]), [("zuz", 0, 1)], [("zuz", 0, 1)])
-    for w in (8, 16, 32):
-        do("S", lambda s: s.activation(T.zu[:, 17:33, w:2 * w], T.zu[:, 17:33, 0:w], Fn.Copy), [("zuu", 0, w)], [("zuu", w, 2 * w)])
-    do("V", lambda v: v.quantize_mx(T.zq[:, 0:272], T.zs[:, 0:272], T.zu[:, 0:17, :]), [("zuz", 0, 1)], [("zq", 0, 272)])
+    def base(s):
+        do("S", lambda e: e.activation(T.bas[:, 128 * s:128 * s + 128], T.bas0[:], Fn.Identity, bias=T.pflt[:, 2 + s:3 + s]),
+           [("bas0", 0, 1), ("pflt", 2 + s, 3 + s)], [("bas", 128 * s, 128 * s + 128)])
 
-    quant("xq", "xs", "xt", 0, 256, 0, 0, 256)
-    quant("xq", "xs", "xt", 256, 256, 1024, 256, 512)
-    quant("xq1", "xs1", "xt", 0, 254, 4, 1, 255)
-    quant("xq1", "xs1", "xt", 254, 258, 1020, 255, 513)
-    do("V", lambda v: v.quantize_mx(T.zq[:, 272:528], T.zs[:, 272:528], T.zu[:, 17:33, :]), [("zuu", 0, 64)], [("zq", 272, 528)])
+    def four(q, r):
+        copy(q, T.zo[:, :, 4 * r:4 * r + 4], T.us[:, :, :], [("us", 0, 1)], [("zo", r, r + 1)])
 
-    sends = []
-    if prev is not None:
-        sends.append((prev, 0, 0, "arrR"))
-    if nxt is not None:
-        sends.append((nxt, TC - HAL, HAL, "arrL"))
-    after("G", [("xq", c0, c0 + HAL) for _, c0, _, _ in sends], [])
-    for plane in (0, 1):
-        tr = []
-        for i, (dst, c0, d0, sem) in enumerate(sends):
-            rid, pid, _ = topo.addr(dst)
-            eng = topo.engines(core, dst)[ENG * i:ENG * i + ENG]
-            s, d = (T.xs[:, c0:c0 + HAL], T.hs[:, d0:d0 + HAL]) if plane else \
-                (T.xq[:, c0:c0 + HAL].bitcast(dt.uint8), T.hq[:, d0:d0 + HAL].bitcast(dt.uint8))
-            tr.append(RemoteDMATransfer(dst_ids=[DstId(rid=rid, pnc=pid)], dma_engine_mask=sum(1 << e for e in eng),
-                                        remote_sem=T.sem[sem], src=s, dst=d))
-        g.remote_dma_fused(tr, local_sem=T.sem.sent)
-    sent = 2 * ENG * len(sends)
+    def among(q, k):
+        copy(q, T.zl[:, 0:8, 32 * k + 16:32 * k + 32], T.zo[:, 8 * k:8 * k + 8, 0:16], [("zo", 0, 4)], [("zl", k, k + 1)])
 
-    after("Y", [("xt", 0, 512)], [])
-    dma("Y", "dwt", T.wt[:], T.w[:], [], [("wt", 0, 1)])
+    def sixteen(q, r):
+        copy(q, T.zo[:, :, 16 * r:16 * r + 16], T.zo[:, :, 0:16], [("zo", 0, 4)], [("zo", 4 * r, 4 * r + 4)])
 
-    def unpack_mm(b):
-        mm(b, TC, "eq", 128 * b, "xq", 0, True, True)
+    def quant_zl():
+        do("V", lambda v: v.quantize_mx(T.zq[:, 0:144], T.zs[:, 0:144], T.zl[:, :, :]), [("zl", 0, 2)], [("zq", 0, 144)])
 
-    def unpack_copy(b):
-        do("S", lambda s: s.activation(T.vw[:, 4 * OWN + b:4 * RGT:4], T.ps[:, 512 * b:512 * b + 512], Fn.Copy),
-           [("ps%d" % b, 0, 512)], [("vw%d" % b, OWN, RGT)])
+    def quant_zo():
+        do("V", lambda v: v.quantize_mx(T.zq[:, 144:400], T.zs[:, 144:400], T.zo[:, :, :]), [("zo", 0, 16)], [("zq", 144, 400)])
 
-    def diff(b):
-        do("V", lambda v: v.tensor_tensor(T.dw[:, 4 * OWN + b:4 * (RGT - 1):4], T.ps[:, 512 * b + 1:512 * b + 512],
-                                          T.vw[:, 4 * OWN + b:4 * (RGT - 1):4], Op.subtract),
-           [("ps%d" % b, 0, 512), ("vw%d" % b, OWN, RGT - 1)], [("dw%d" % b, OWN, RGT - 1)])
+    def send():
+        sends = []
+        if prev is not None:
+            sends.append((prev, 0, HAL, "arrR"))
+        if nxt is not None:
+            sends.append((nxt, TC - HAL, 0, "arrL"))
+        after("G", [("xq", c0, c0 + HAL) for _, c0, _, _ in sends], [])
+        for plane in (0, 1):
+            tr = []
+            for i, (dst, c0, d0, sem) in enumerate(sends):
+                rid, pid, _ = topo.addr(dst)
+                eng = topo.engines(core, dst)[ENG * i:ENG * i + ENG]
+                s, d = (T.xs[:, c0:c0 + HAL], T.hs[:, d0:d0 + HAL]) if plane else \
+                    (T.xq[:, c0:c0 + HAL].bitcast(dt.uint8), T.hq[:, d0:d0 + HAL].bitcast(dt.uint8))
+                tr.append(RemoteDMATransfer(dst_ids=[DstId(rid=rid, pnc=pid)], dma_engine_mask=sum(1 << e for e in eng),
+                                            remote_sem=T.sem[sem], src=s, dst=d))
+            g.remote_dma_fused(tr, local_sem=T.sem.sent)
+        return 2 * ENG * len(sends)
+
+    def unpack_copy(b, p0, w0, n, q="S"):
+        copy(q, T.vw[:, 4 * w0 + b:4 * (w0 + n):4], T.ps[:, 512 * b + p0:512 * b + p0 + n], bank(b), [("vw%d" % b, w0, w0 + n)])
+
+    def diff(b, p0, w0, lo, hi):
+        p = 512 * b + p0 - w0 + 1
+        do("V", lambda v: v.tensor_tensor(T.dw[:, 4 * lo + b:4 * hi:4], T.ps[:, p + lo:p + hi], T.vw[:, 4 * lo + b:4 * hi:4], Op.subtract),
+           bank(b) + [("vw%d" % b, lo, hi)], [("dw%d" % b, lo, hi)])
+
+    def list_mm(s):
+        for h in range(2):
+            mm(6 + s, 128, "zq", 4 - 4 * h, "xq", RUNS[s][h], h == 0, h == 1)
+
+    def whole(q, s, k):
+        for j0, n, at in [(128, 256, 0)] if s == A else [(0, 128, 0), (384, 128, 128)]:
+            at += 512 * s + 256 * k
+            d = T.ps[:, 512 * (4 + k) + j0:512 * (4 + k) + j0 + n]
+            if q == "V":
+                do(q, lambda v: v.tensor_scalar(T.rn[:, at:at + n], d, MAGIC, -MAGIC, Op.add, Op.add), bank(4 + k), [("rn", at, at + n)])
+            else:
+                do(q, lambda e: e.activation(T.tm[:, at:at + n], d, Fn.Copy, bias=MAGIC), bank(4 + k), [("tm", at, at + n)])
+
+    def whole2(lo, hi):
+        do("S", lambda e: e.activation(T.rn[:, lo:hi], T.tm[:, lo:hi], Fn.Copy, bias=-MAGIC), [("tm", lo, hi)], [("rn", lo, hi)])
+
+    def frac(s, k):
+        for h in range(2):
+            a, at, p = 2 * k + h, 512 * s + 256 * k + 128 * h, 512 * (4 + k) + RUNS[s][h]
+            do("V", lambda v: v.tensor_tensor(T.fr[:, 2048 * s + 4 * a:2048 * s + 2048:16], T.ps[:, p:p + 128], T.rn[:, at:at + 128], Op.subtract),
+               bank(4 + k) + [("rn", at, at + 128)], [("fr0%d" % a, 512 * s, 512 * s + 512)])
+
+    def spread(q, lo, hi, bs):
+        for b in bs:
+            copy(q, T.fr[:, 4 * lo + b:4 * hi:4], T.fr[:, 4 * lo:4 * hi:4], each("fr0", lo, hi), [("fr%d" % b, lo, hi)])
+
+    def inside(s):
+        at = (128 * s, 128 * s + 128)
+        ab, sg = T.ab[:, at[0]:at[1]], T.sg[:, at[0]:at[1]]
+        return [lambda: do("S", lambda e: e.activation(ab, T.ps[:, 512 * (6 + s):512 * (6 + s) + 128], Fn.Abs), bank(6 + s), [("ab", *at)]),
+                lambda: do("S", lambda e: e.activation(sg, ab, Fn.Sign, bias=float(CL), scale=-1.0), [("ab", *at)], [("sg", *at)])]
+
+    def lists(s):
+        lo, hi = 128 * s, 128 * s + 128
+        ni, pl, sg, dp, vl, dl, bas = (T[n][:, lo:hi] for n in ("ni", "pl", "sg", "dp", "vl", "dl", "bas"))
+        key = lambda *n: [(m, lo, hi) for m in n]
+        d, b = T.ps[:, 512 * (6 + s):512 * (6 + s) + 128], T.pflt[:, 0:1]
+
+        def place():
+            do("V", lambda v: v.tensor_tensor(pl, ni, bas, Op.add), key("ni", "bas"), key("pl"))
+            if s == E and prev is None:
+                do("V", lambda v: v.tensor_scalar(pl, pl, float(OWN - first[s]), None, Op.max), key("pl"), key("pl"))
+            if s == E and nxt is None:
+                do("V", lambda v: v.tensor_scalar(pl, pl, float(RGT - 1 - first[s]), None, Op.min), key("pl"), key("pl"))
+        return [
+            lambda: do("V", lambda v: v.tensor_scalar(ni, d, float(-CL), float(CL), Op.max, Op.min), bank(6 + s), key("ni")),
+            place,
+            lambda: do("V", lambda v: v.tensor_scalar(vl, pl, 4.0, b, Op.mult, Op.add), key("pl") + [("pflt", 0, 1)], key("vl")),
+            lambda: do("V", lambda v: v.tensor_tensor(dp, pl, sg, Op.mult), key("pl", "sg"), key("dp")),
+            lambda: do("V", lambda v: v.tensor_scalar(dl, dp, 4.0, b, Op.mult, Op.add), key("dp") + [("pflt", 0, 1)], key("dl"))]
+
+    def window(name, lo, hi):
+        s = lo // 512
+        last = end[s] - (name == "dw" and (s == A or nxt is not None))
+        lst = "dl" if name == "dw" else "vl"
+        return T[name][:, 4 * first[s]:4 * last].indirect(T[lst][:, lo // 4:hi // 4]), each(name, first[s], last) + [(lst, 128 * s, 128 * s + 128)]
+
+    def slope(lo, hi):
+        win, reads = window("dw", lo, hi)
+        do("V", lambda v: v.tensor_tensor(T.pp[:, 4 * lo:4 * hi], win, T.fr[:, 4 * lo:4 * hi], Op.mult),
+           reads + each("fr0", lo, hi) + each("fr", lo, hi, (1, 2, 3)), [("pp", lo, hi)])
+
+    def tap(lo, hi):
+        win, reads = window("vw", lo, hi)
+        do("V", lambda v: v.tensor_tensor(T.mt[:, 4 * lo:4 * hi], win, T.pp[:, 4 * lo:4 * hi], Op.add), reads + [("pp", lo, hi)], [("mt", lo, hi)])
+
+    def far_v(lo, hi):
+        win, reads = window("vw", lo, hi)
+        do("S", lambda e: e.activation(T.mt[:, 4 * lo:4 * hi], win, Fn.Copy), reads, [("mt", lo, hi)])
+
+    adds = [0]
+
+    def far_add(lo, hi):
+        dma("G", "da%d" % adds[0], T.mt[:, 4 * lo:4 * hi], T.pp[:, 4 * lo:4 * hi], [("pp", lo, hi), ("mt", lo, hi)], [("mt", lo, hi)], accum_op=Op.add)
+        adds[0] += 1
+
+    def quant_m(lo, hi):
+        quant("mq", "ms", "mt", lo, hi - lo, 4 * lo, lo, hi)
+
+    stores = [0]
+
+    def products(lo, hi, banks):
+        for o in range(2):
+            for k in range(2):
+                mm(banks[o], hi - lo - 2, "wq", 128 * (2 * k + o), "mq", lo + 2 * k, k == 0, k == 1)
+
+    def to_y(lo, hi, banks, qs, blocks=(0, 1)):
+        s, c0, n = lo // 512, lo % 512 // 4, (hi - lo) // 4
+        for o in blocks:
+            for h in range(2):
+                j = TC * o + RUNS[s][h] + c0
+                copy(qs[2 * o + h], T.yb[:, j:j + n], T.ps[:, 512 * banks[o] + h:512 * banks[o] + 4 * n - 2:4], bank(banks[o]), [("yb", j, j + n)])
+
+    def store(q, j0, j1):
+        dma(q, "dy%d" % stores[0], T.y[:, j0:j1], T.yb[:, j0:j1], [("yb", j0, j1)], [])
+        stores[0] += 1
+
+    H2 = OWN + 256
+    h0, h1 = (0 if prev is not None else HAL), (2 * HAL if nxt is not None else HAL)
+
+    def halo_mm():
+        for b in range(4):
+            mm(b, h1 - h0, "eq", 128 * b, "hq", h0, True, True)
+
+    def hc(b, q="SS"):
+        if prev is not None:
+            unpack_copy(b, 0, 0, HAL, q[0])
+        if nxt is not None:
+            unpack_copy(b, HAL - h0, RGT, HAL, q[1])
+
+    def hd(b):
+        if prev is not None:
+            diff(b, 0, 0, 1, HAL - 1)
+        if nxt is not None:
+            diff(b, HAL - h0, RGT, RGT - 1, WIN - 1)
+
+    def halo(b):
+        hc(b); hd(b)
+
+    def quant_x(half):
+        quant("xq", "xs", "xt", 256 * half, 256, 1024 * half, 256 * half, 256 * half + 256)
+
+    def quant_w():
+        quant("wq", "ws", "wt", 0, 512, 0, 0, 1)
+
+    def seam():
+        lo = OWN - 1 if prev is not None else OWN
+        do("V", lambda v: v.tensor_tensor(T.dw[:, 4 * lo:4 * OWN + 4], T.vw[:, 4 * lo + 4:4 * OWN + 8], T.vw[:, 4 * lo:4 * OWN + 4], Op.subtract),
+           each("vw", lo, OWN + 2), each("dw", lo, OWN + 1))
+
+    c1 = lambda b, q="S": unpack_copy(b, 0, OWN, 256, q)
+    d1 = lambda b: diff(b, 0, OWN, OWN + 1, OWN + 255)
+    c2 = lambda b, q="S": unpack_copy(b, 0, H2, 256, q)
+    d2 = lambda b: diff(b, 0, H2, H2 - 1, RGT - 1)
+    la, ia, le, ie = lists(A), inside(A), lists(E), inside(E)
+
+    def load_w():
+        after("Y", [("xt", 0, 512)], [])
+        dma("Y", "dwt", T.wt[:], T.w[:], [], [("wt", 0, 1)])
 
     def offs_mm(k):
-        mm(6 + k, TC, "zq", 272 + 128 * k, "xq", 0, True, True)
+        mm(4 + k, TC, "zq", 144 + 128 * k, "xq", 0, True, True)
 
-    def list_mm(k):
-        for n, a in enumerate((0, 2, 1, 3)):
-            mm(4 + k, 510, "zq", 128 * k + 12 - 4 * a, "xq1" if a % 2 else "xq", a - a % 2, n == 0, n == 3)
-
-    def frac_n(k, j0, j1):
-        do("S", lambda s: s.activation(T["tm%d" % k][:, j0:j1], T.ps[:, 512 * (6 + k) + j0:512 * (6 + k) + j1], Fn.Copy, bias=MAGIC),
-           [("ps%d" % (6 + k), 0, 512)], [("tm%d" % k, j0, j1)])
-        do("S", lambda s: s.activation(T["rn%d" % k][:, j0:j1], T["tm%d" % k][:, j0:j1], Fn.Copy, bias=-MAGIC),
-           [("tm%d" % k, j0, j1)], [("rn%d" % k, j0, j1)])
-
-    def frac_sub(k, j0, j1):
-        do("V", lambda v: v.tensor_tensor(T["fr%d" % k][:, 4 * j0:4 * j1:4], T.ps[:, 512 * (6 + k) + j0:512 * (6 + k) + j1],
-                                          T["rn%d" % k][:, j0:j1], Op.subtract),
-           [("ps%d" % (6 + k), 0, 512), ("rn%d" % k, j0, j1)], [("fr%d0" % k, j0, j1)])
-
-    def frac_rep(q, k, j0, j1, bs):
+    def unpack_mm(half, bs=range(4)):
         for b in bs:
-            out, in_ = T["fr%d" % k][:, 4 * j0 + b:4 * j1:4], T["fr%d" % k][:, 4 * j0:4 * j1:4]
-            call = {"S": lambda s: s.activation(out, in_, Fn.Copy), "V": lambda v: v.tensor_copy(out, in_),
-                    "G": lambda e: e.affine_select(out, in_, [[1, j1 - j0]], Op.is_gt, 0.0, 1, 0)}[q]
-            do(q, call, [("fr%d0" % k, j0, j1)], [("fr%d%d" % (k, b), j0, j1)])
+            mm(b, 256, "eq", 128 * b, "xq", 256 * half, True, True)
 
-    def inside(k):
-        ab, sg = T["ab%d" % k], T["sg%d" % k]
-        do("S", lambda s: s.activation(ab[:], T.ps[:, 512 * (4 + k):512 * (4 + k) + 509:4], Fn.Abs), [("ps%d" % (4 + k), 0, 512)], [("ab%d" % k, 0, 128)])
-        do("S", lambda s: s.activation(sg[:], ab[:], Fn.Sign, bias=float(CL), scale=-1.0), [("ab%d" % k, 0, 128)], [("sg%d" % k, 0, 128)])
-
-    def lists(k):
-        ni, pl, wr, sg, dp, vl, dl = (T[n + str(k)] for n in ("ni", "pl", "wr", "sg", "dp", "vl", "dl"))
-        key = lambda n, lo=0, hi=128: (n + str(k), lo, hi)
-        d = T.ps[:, 512 * (4 + k):512 * (4 + k) + 509:4]
-        do("V", lambda v: v.tensor_scalar(ni[:], d, float(-CL), float(CL), Op.max, Op.min), [("ps%d" % (4 + k), 0, 512)], [key("ni")])
-        do("V", lambda v: v.tensor_tensor(pl[:], ni[:], T.bas[:], Op.add), [key("ni"), ("bas", 0, 1)], [key("pl")])
-        if prev is None:
-            do("V", lambda v: v.tensor_scalar(pl[:, 0:32], pl[:, 0:32], float(OWN), None, Op.max), [key("pl", 0, 32)], [key("pl", 0, 32)])
-        else:
-            do("V", lambda v: v.tensor_scalar(wr[:], pl[:, 0:32], float(OWN), float(WIN - OWN), Op.is_lt, Op.mult), [key("pl", 0, 32)], [key("wr")])
-            do("V", lambda v: v.tensor_tensor(pl[:, 0:32], pl[:, 0:32], wr[:], Op.add), [key("pl", 0, 32), key("wr")], [key("pl", 0, 32)])
-        if nxt is None:
-            do("V", lambda v: v.tensor_scalar(pl[:, 96:128], pl[:, 96:128], float(RGT - 1), None, Op.min), [key("pl", 96, 128)], [key("pl", 96, 128)])
-        do("V", lambda v: v.tensor_scalar(vl[:], pl[:], 4.0, T.pflt[:, 0:1], Op.mult, Op.add), [key("pl"), ("pflt", 0, 1)], [key("vl")])
-        do("V", lambda v: v.tensor_tensor(dp[:], pl[:], sg[:], Op.mult), [key("pl"), key("sg")], [key("dp")])
-        do("V", lambda v: v.tensor_scalar(dl[:], dp[:], 4.0, T.pflt[:, 0:1], Op.mult, Op.add), [key("dp"), ("pflt", 0, 1)], [key("dl")])
-
-    def slope(k, j0, j1, end):
-        do("V", lambda v: v.tensor_tensor(T["pp%d" % k][:, 4 * j0:4 * j1], T.dw[:, 0:4 * end].indirect(T["dl%d" % k][:, j0 // 4:j1 // 4]),
-                                          T["fr%d" % k][:, 4 * j0:4 * j1], Op.mult),
-           [("dw%d" % b, 0, end) for b in range(4)] + [("fr%d%d" % (k, b), j0, j1) for b in range(4)] + [("dl%d" % k, 0, 128)],
-           [("pp%d" % k, j0, j1)])
-
-    def tap(k, j0, j1, end):
-        do("V", lambda v: v.tensor_tensor(T["mt%d" % k][:, 4 * j0:4 * j1], T.vw[:, 0:4 * end].indirect(T["vl%d" % k][:, j0 // 4:j1 // 4]),
-                                          T["pp%d" % k][:, 4 * j0:4 * j1], Op.add),
-           [("vw%d" % b, 0, end) for b in range(4)] + [("pp%d" % k, j0, j1), ("vl%d" % k, 0, 128)], [("mt%d" % k, j0, j1)])
-
-    def far_v(k, j0, j1, end):
-        do("S", lambda s: s.activation(T["mt%d" % k][:, 4 * j0:4 * j1], T.vw[:, 0:4 * end].indirect(T["vl%d" % k][:, j0 // 4:j1 // 4]), Fn.Copy),
-           [("vw%d" % b, 0, end) for b in range(4)] + [("vl%d" % k, 0, 128)], [("mt%d" % k, j0, j1)])
-
-    def far_add(k, j0, j1, sem):
-        dma("G", sem, T["mt%d" % k][:, 4 * j0:4 * j1], T["pp%d" % k][:, 4 * j0:4 * j1],
-            [("pp%d" % k, j0, j1), ("mt%d" % k, j0, j1)], [("mt%d" % k, j0, j1)], accum_op=Op.add)
-
-    def finish(j0, j1, banks, n, first=0, last=False):
-        for k in (first, 1 - first):
-            quant("mq%d" % k, "ms%d" % k, "mt%d" % k, j0, j1 - j0, 4 * j0, j0, j1)
-            for o in range(2):
-                mm(banks[o], j1 - j0, "wq", 128 * (2 * k + o), "mq%d" % k, j0, k == first, k != first)
-        for o in range(2):
-            src, dst = T.ps[:, 512 * banks[o]:512 * banks[o] + j1 - j0], T.yb[:, TC * o + j0:TC * o + j1]
-            acc = ([("ps%d" % banks[o], 0, 512)], [("yb%d" % o, j0, j1)])
-            if last and o == 1:
-                do("V", lambda v: v.tensor_copy(dst, src), *acc)
-            else:
-                do("S", lambda s: s.activation(dst, src, Fn.Copy), *acc)
-            dma("S" if last and o == 1 else "Y", "dy%d" % (2 * n + o), T.y[:, TC * o + j0:TC * o + j1], dst, [("yb%d" % o, j0, j1)], [])
-
-    A, LO, HI = (128, 384), (0, 128), (384, 512)
-    unpack_mm(0); unpack_mm(1); offs_mm(0); list_mm(0)
-    unpack_copy(0); unpack_copy(1)
-    frac_n(0, *A); frac_n(0, *LO); frac_n(0, *HI)
-    diff(0); diff(1); frac_sub(0, *A); frac_rep("S", 0, *A, (1, 2)); frac_rep("V", 0, *A, (3,))
-    unit_q(2); unit_q(3)
-    unpack_mm(2); unpack_mm(3); offs_mm(1); list_mm(1)
-    frac_sub(0, *LO); frac_sub(0, *HI); frac_rep("G", 0, *LO, (2, 3)); frac_rep("G", 0, *HI, (2, 3))
-    inside(0); unpack_copy(2); unpack_copy(3); lists(0)
-    diff(2); diff(3)
-    frac_n(1, 0, TC)
-    slope(0, *A, RGT - 1)
-    far_v(0, *A, RGT)
-    frac_sub(1, 0, TC)
-    inside(1)
-    frac_rep("G", 1, *A, (3,)); frac_rep("S", 1, *A, (1, 2))
-    far_add(0, *A, "da0")
-    frac_rep("G", 1, *LO, (3,)); frac_rep("G", 1, *HI, (3,))
-    lists(1)
-    slope(1, *A, RGT - 1)
-    far_v(1, *A, RGT); far_add(1, *A, "da1")
-
-    h0, h1 = (0 if nxt is not None else HAL), (2 * HAL if prev is not None else HAL)
-    w0, w1 = RGT + h0, RGT + h1
-    e = 1 if nxt is None else 0
+    quant_e(1); quant_e(2); quant_e(3); base(A); base(E)
+    four("V", 0); four("V", 1); four("V", 2); four("S", 3); sixteen("S", 1); sixteen("S", 2)
+    among("V", 0); among("V", 1)
+    quant_x(0); unpack_mm(0)
+    sixteen("V", 3); quant_zl()
+    quant_x(1); sent = send(); load_w()
+    quant_zo(); list_mm(A); list_mm(E); offs_mm(0); offs_mm(1)
     for b in range(4):
-        mm(b, h1 - h0, "eq", 128 * b, "hq", h0, True, True)
-    for b in range(4):
-        do("S", lambda s: s.activation(T.vw[:, 4 * w0 + b:4 * w1:4], T.ps[:, 512 * b:512 * b + w1 - w0], Fn.Copy),
-           [("ps%d" % b, 0, 512)], [("vw%d" % b, w0, w1)])
-        do("V", lambda v: v.tensor_tensor(T.dw[:, 4 * (w0 - 1 + e) + b:4 * (w1 - 1):4], T.ps[:, 512 * b + e:512 * b + w1 - w0],
-                                          T.vw[:, 4 * (w0 - 1 + e) + b:4 * (w1 - 1):4], Op.subtract),
-           [("ps%d" % b, 0, 512), ("vw%d" % b, w0 - 1 + e, w1 - 1)], [("dw%d" % b, w0 - 1 + e, w1 - 1)])
-    if prev is not None:
-        do("V", lambda v: v.tensor_tensor(T.dw[:, 4 * (WIN - 1):4 * WIN], T.vw[:, 4 * OWN:4 * OWN + 4], T.vw[:, 4 * (WIN - 1):4 * WIN], Op.subtract),
-           [("vw%d" % b, OWN, OWN + 1) for b in range(4)] + [("vw%d" % b, WIN - 1, WIN) for b in range(4)],
-           [("dw%d" % b, WIN - 1, WIN) for b in range(4)])
-    frac_rep("S", 0, *LO, (1,)); frac_rep("S", 0, *HI, (1,)); frac_rep("S", 1, *LO, (1, 2)); frac_rep("S", 1, *HI, (1, 2))
+        c1(b); d1(b)
+    unpack_mm(1)
 
-    L = LO + ((RGT - 1, RGT) if prev is None else (WIN, WIN))
-    R = HI + ((LFT - 1, LFT) if nxt is not None else (RGT, RGT))
-    E1, E2 = (L, R) if prev is None else (R, L)
-    slope(0, *E1[:3]); far_v(0, *E1[:2], E1[3]); far_add(0, *E1[:2], "da2")
-    slope(0, *E2[:3]); far_v(0, *E2[:2], E2[3]); far_add(0, *E2[:2], "da3")
-    slope(1, *E1[:3]); slope(1, *E2[:3])
-    tap(1, *E1[:2], E1[3])
-    quant("wq", "ws", "wt", 0, 512, 0, 0, 1)
-    finish(*A, (4, 5), 0)
-    finish(*E1[:2], (6, 7), 1)
-    tap(1, *E2[:2], E2[3])
-    finish(*E2[:2], (0, 1), 2, first=1, last=True)
+    ia[0](); la[0](); ie[0](); whole("S", A, 0); ia[1](); whole2(0, 256)
+    whole("V", A, 1); la[1](); le[0](); la[2](); frac(A, 1); la[3](); frac(A, 0); la[4]()
+    c2(0); c2(1); c2(2); c2(3)
+    whole("V", E, 0); whole("V", E, 1)
+    spread("S", 0, 256, (1, 2, 3)); spread("G", 256, 512, (2, 3)); spread("S", 256, 512, (1,))
+    d2(0); d2(1); frac(E, 0); frac(E, 1); d2(2); d2(3)
+
+    slope(0, 256); ie[1](); far_v(0, 256)
+    spread("G", 512, 768, (1, 2)); far_add(0, 256)
+    slope(256, 512); far_v(256, 512)
+    spread("G", 512, 768, (3,)); far_add(256, 512); spread("G", 768, 1024, (1, 2, 3))
+    halo_mm()
+    le[1](); quant_w(); le[2](); le[3]()
+    halo(0); le[4](); halo(1); halo(2); halo(3); seam()
+
+    P1, P2 = 752, 888
+    c = (P1 - TC) // 4
+    slope(TC, P1); far_v(TC, P1); far_add(TC, P1)
+    slope(P1, P2); far_v(P1, P2); far_add(P1, P2)
+    quant_m(0, TC); products(0, TC, (4, 5))
+    slope(P2, 2 * TC)
+    for o in range(2):
+        to_y(0, TC, (4, 5), "SSSS", (o,)); store("Y", TC * o + 128, TC * o + 384)
+    quant_m(TC, P1); products(TC, P1, (6, 7))
+    tap(P2, 2 * TC)
+    for o in range(2):
+        to_y(TC, P1, (6, 7), "SSSS", (o,)); store("Y", TC * o, TC * o + c); store("Y", TC * o + 384, TC * o + 384 + c)
+    quant_m(P1, 2 * TC); products(P1, 2 * TC, (2, 3))
+    for o in range(2):
+        to_y(P1, 2 * TC, (2, 3), "VVVV", (o,)); store("Y", TC * o + c, TC * o + 128); store("S", TC * o + 384 + c, TC * o + TC)
     g.wait_ge(T.sem.sent, sent)
     drain("Y")

@@ -5,10 +5,12 @@ N, TC, CL = 4, 512, 127
 HAL = 128
 OWN, RGT, WIN = 128, 640, 768
 MAGIC = 12582912.0
-A, E = 0, 1
-RUNS = ((128, 256), (0, 384))
+A, LO, HI = 0, 1, 2
+RUNS = ((128, 256), (0, 64), (384, 448))
+WIDE = (128, 64, 64)
+AT = (0, 512, 768, 1024)
 
-F32, BF, U16, I32 = "float32", "bfloat16", "uint16", "int32"
+F32, BF, F16, U16, I32 = "float32", "bfloat16", "float16", "uint16", "int32"
 X4 = "float8_e4m3fn_x4"
 SCRATCH = {
     "xt": ("sbuf", [128, 4 * TC], BF),
@@ -20,24 +22,23 @@ SCRATCH = {
     "unit": ("sbuf", [128, 528], BF),
     "pidx": ("sbuf", [128, 2], I32),
     "pint": ("sbuf", [128, 4], I32),
-    "pflt": ("sbuf", [128, 4], F32),
-    "bas0": ("sbuf", [128, 128], F32),
+    "pflt": ("sbuf", [128, 8], F32),
     "xq": ("sbuf", [128, TC], X4), "xs": ("sbuf", [128, TC], "uint8"),
     "zq": ("sbuf", [128, 400], X4), "zs": ("sbuf", [128, 400], "uint8"),
     "eq": ("sbuf", [128, 512], X4), "es": ("sbuf", [128, 512], "uint8"),
     "wq": ("sbuf", [128, 512], X4), "ws": ("sbuf", [128, 512], "uint8"),
     "hq": ("sbuf", [128, 2 * HAL], X4), "hs": ("sbuf", [128, 2 * HAL], "uint8"),
-    "mq": ("sbuf", [128, 2 * TC], X4), "ms": ("sbuf", [128, 2 * TC], "uint8"),
+    "mq": ("sbuf", [128, 2 * TC + 2], X4), "ms": ("sbuf", [128, 2 * TC + 2], "uint8"),
     "vw": ("sbuf", [128, 4 * WIN], F32), "dw": ("sbuf", [128, 4 * WIN], F32),
     "tm": ("sbuf", [128, 2 * TC], F32), "rn": ("sbuf", [128, 2 * TC], F32),
-    "fr": ("sbuf", [128, 8 * TC], F32), "pp": ("sbuf", [128, 8 * TC], F32), "mt": ("sbuf", [128, 8 * TC], BF),
-    "bas": ("sbuf", [128, 256], F32), "ni": ("sbuf", [128, 256], I32), "pl": ("sbuf", [128, 256], I32),
-    "dp": ("sbuf", [128, 256], I32), "ab": ("sbuf", [128, 256], F32), "sg": ("sbuf", [128, 256], F32),
+    "fr": ("sbuf", [128, 8 * TC], F32), "pp": ("sbuf", [128, 8 * TC], F32), "mt": ("sbuf", [128, 8 * TC + 8], BF),
+    "bas": ("sbuf", [128, 256], I32), "ni": ("sbuf", [128, 256], I32), "pl": ("sbuf", [128, 256], F16),
+    "dp": ("sbuf", [128, 256], F16), "ab": ("sbuf", [128, 256], F32), "sg": ("sbuf", [128, 256], F32),
     "vl": ("sbuf", [128, 256], U16), "dl": ("sbuf", [128, 256], U16),
     "yb": ("sbuf", [128, 2 * TC], F32),
     "ps": ("psum", [128, 4096], F32),
 }
-SEMAPHORES = ["cV", "cS", "cP", "cG", "sent", "arrR", "arrL", "dx1", "dx2", "du", "dwt"] + \
+SEMAPHORES = ["cV", "cS", "cP", "cG", "sent", "arrR", "arrL", "dx0", "dx1", "dx2", "dx3", "du", "dwt"] + \
     ["dy%d" % i for i in range(12)] + ["da%d" % i for i in range(6)]
 
 Op, Fn = AluOpType, ActivationFunctionType
@@ -59,7 +60,7 @@ def scheduler(g, T):
                     bank = key[:2] == "ps"
                     if mine == "r" and kind == "r" and not (bank and oq != q):
                         continue
-                    if src == "c" + q and (kind == "r" or bank):
+                    if src == "c" + q and bank:
                         continue
                     deps[src] = max(deps.get(src, 0), t)
         for src, t in list(deps.items()):
@@ -116,8 +117,8 @@ def rank_program(g, core, T, topo):
         arrival("arrL", 2 * ENG, [("hq", 0, HAL)])
     if nxt is not None:
         arrival("arrR", 2 * ENG, [("hq", HAL, 2 * HAL)])
-    first = (OWN, 0 if prev is not None else OWN - 2)
-    end = (RGT, WIN if nxt is not None else RGT)
+    first = (OWN,) + 2 * (0 if prev is not None else OWN - 2,)
+    end = (RGT, RGT, WIN if nxt is not None else RGT)
     each = lambda name, lo, hi, bs=range(4): [("%s%d" % (name, b), lo, hi) for b in bs]
     bank = lambda n: [("ps%d" % n, 0, 512)]
 
@@ -134,29 +135,29 @@ def rank_program(g, core, T, topo):
 
     def copy(q, out, in_, reads, writes):
         if q == "G":
-            do(q, lambda e: e.affine_select(out, in_, [[1, out.shape[1]]], Op.is_gt, 0.0, 1, 0), reads, writes)
+            do(q, lambda e: e.affine_select(out, in_, [[1, n] for n in out.shape[1:]], Op.is_gt, 0.0, 1, 0), reads, writes)
         else:
             do(q, lambda e: e.activation(out, in_, Fn.Copy) if q == "S" else e.tensor_copy(out, in_), reads, writes)
 
-    dma("Y", "dx1", T.xt[:, 0:1024], T.x[:, 0:1024], [], [("xt", 0, 256)])
     dma("S", "du", T.us[:, :, :], T.u[:, 0:64], [], [("us", 0, 1)])
-    dma("Y", "dx2", T.xt[:, 1024:2048], T.x[:, 1024:2048], [], [("xt", 256, 512)])
+    for q, i in (("Y", 0), ("S", 3), ("Y", 1), ("S", 2)):
+        dma(q, "dx%d" % i, T.xt[:, 512 * i:512 * i + 512], T.x[:, 512 * i:512 * i + 512], [], [("xt", 128 * i, 128 * i + 128)])
 
     do("G", lambda e: e.iota(T.pidx[:, 0:1], [[0, 1]], 0, 1), [], [("pidx", 0, 1)])
+    do("G", lambda e: e.iota(T.bas[:, 0:128], [[1, 128]], OWN + RUNS[A][0] - first[A] + 4 * WIDE[A] + 1, 0), [], [("bas", 0, 128)])
     do("V", lambda v: v.memset(T.ones[:], 1.0), [], [("ones", 0, 1)])
     do("V", lambda v: v.memset(T.unit[:], 0.0), [], [("unit", 0, 1)])
     do("G", lambda e: e.affine_select(T.unit[:, 3:515:4], T.ones[:], [[-1, 128]], Op.is_equal, 0.0, 0, 1),
        [("ones", 0, 1)], [("unit", 0, 1)])
     do("V", lambda v: v.memset(T.zl[:, :, :], 0.0), [], [("zl", 0, 2)])
-    whole_numbers = lambda out, step: lambda e: e.iota(out, [[step, out.shape[1]]], 0, 0, allow_small_or_imprecise_dtypes=True)
-    do("G", whole_numbers(T.bas0[:], 1), [], [("bas0", 0, 1)])
-    zeros = [("dw", OWN, OWN + 1), ("dw", first[E], first[E] + 1)]
+    do("G", lambda e: e.iota(T.bas[:, 128:256], [[RUNS[HI][0], 2], [1, 64]], OWN - first[LO] + 4 * WIDE[LO] + 1, 0), [], [("bas", 128, 256)])
+    zeros = [("dw", OWN, OWN + 1), ("dw", first[LO], first[LO] + 1)]
     if prev is None:
         zeros = [("dw", OWN - 2, OWN + 1), ("vw", OWN - 2, OWN)]
     if nxt is None:
         zeros.append(("dw", RGT - 1, RGT))
     for w, lo, hi in zeros:
-        do("G", whole_numbers(T[w][:, 4 * lo:4 * hi], 0), [], each(w, lo, hi))
+        do("G", lambda e: e.iota(T[w][:, 4 * lo:4 * hi], [[0, 4 * (hi - lo)]], 0, 0, allow_small_or_imprecise_dtypes=True), [], each(w, lo, hi))
     do("V", lambda v: v.tensor_scalar(T.pint[:, 0:1], T.pidx[:, 0:1], 3, None, Op.bitwise_and), [("pidx", 0, 1)], [("pint", 0, 1)])
     do("V", lambda v: v.tensor_scalar(T.pint[:, 1:2], T.pidx[:, 0:1], 2, 1, Op.arith_shift_right, Op.bitwise_and),
        [("pidx", 0, 1)], [("pint", 1, 2)])
@@ -165,14 +166,15 @@ def rank_program(g, core, T, topo):
         quant("eq", "es", "unit", 128 * b, 128, 3 - b, 0, 1)
 
     quant_e(0)
-    do("V", lambda v: v.tensor_copy(T.pflt[:, 0:2], T.pint[:, 0:2]), [("pint", 0, 2)], [("pflt", 0, 1)])
-    for s in (A, E):
-        do("S", lambda e: e.activation(T.pflt[:, 2 + s:3 + s], T.pflt[:, 1:2], Fn.Copy, bias=float(OWN + RUNS[s][0] - first[s]),
-                                       scale=float(RUNS[s][1] - RUNS[s][0])), [("pflt", 0, 1)], [("pflt", 2 + s, 3 + s)])
+    do("V", lambda v: v.tensor_scalar(T.pflt[:, 0:2], T.pint[:, 0:2], -4.0, None, Op.add), [("pint", 0, 2)], [("pflt", 0, 1)])
 
-    def base(s):
-        do("S", lambda e: e.activation(T.bas[:, 128 * s:128 * s + 128], T.bas0[:], Fn.Identity, bias=T.pflt[:, 2 + s:3 + s]),
-           [("bas0", 0, 1), ("pflt", 2 + s, 3 + s)], [("bas", 128 * s, 128 * s + 128)])
+    def shift(s):
+        do("S", lambda e: e.activation(T.pflt[:, 2 + s:3 + s], T.pflt[:, 1:2], Fn.Identity, bias=T.pflt[:, 0:1], scale=4.0 * WIDE[s]),
+           [("pflt", 0, 1)], [("pflt", 2 + s, 3 + s)])
+        if s == LO and None in (prev, nxt):
+            edge = OWN - first[LO] + 1 if prev is None else RGT - first[HI]
+            do("S", lambda e: e.activation(T.pflt[:, 4:5], T.pflt[:, 1:2], Fn.Copy, bias=float(edge), scale=-float(WIDE[s])),
+               [("pflt", 0, 1)], [("pflt", 4, 5)])
 
     def four(q, r):
         copy(q, T.zo[:, :, 4 * r:4 * r + 4], T.us[:, :, :], [("us", 0, 1)], [("zo", r, r + 1)])
@@ -216,62 +218,67 @@ def rank_program(g, core, T, topo):
         do("V", lambda v: v.tensor_tensor(T.dw[:, 4 * lo + b:4 * hi:4], T.ps[:, p + lo:p + hi], T.vw[:, 4 * lo + b:4 * hi:4], Op.subtract),
            bank(b) + [("vw%d" % b, lo, hi)], [("dw%d" % b, lo, hi)])
 
+    LB = (6, 7, 6)
+    skip = lambda s: 128 - WIDE[s] if s == HI else 0
+
     def list_mm(s):
         for h in range(2):
-            mm(6 + s, 128, "zq", 4 - 4 * h, "xq", RUNS[s][h], h == 0, h == 1)
+            mm(LB[s], 128, "zq", 4 - 4 * h, "xq", RUNS[s][h] - skip(s), h == 0, h == 1)
 
-    def whole(q, s, k):
-        for j0, n, at in [(128, 256, 0)] if s == A else [(0, 128, 0), (384, 128, 128)]:
-            at += 512 * s + 256 * k
-            d = T.ps[:, 512 * (4 + k) + j0:512 * (4 + k) + j0 + n]
-            if q == "V":
-                do(q, lambda v: v.tensor_scalar(T.rn[:, at:at + n], d, MAGIC, -MAGIC, Op.add, Op.add), bank(4 + k), [("rn", at, at + n)])
-            else:
-                do(q, lambda e: e.activation(T.tm[:, at:at + n], d, Fn.Copy, bias=MAGIC), bank(4 + k), [("tm", at, at + n)])
+    def whole(q, k, j0, j1):
+        j, n = 512 * k + j0, j1 - j0
+        d = T.ps[:, 2048 + j:2048 + j + n]
+        if q == "V":
+            do(q, lambda v: v.tensor_scalar(T.rn[:, j:j + n], d, MAGIC, -MAGIC, Op.add, Op.add), bank(4 + k), [("rn", j, j + n)])
+        else:
+            do(q, lambda e: e.activation(T.tm[:, j:j + n], d, Fn.Copy, bias=MAGIC), bank(4 + k), [("tm", j, j + n)])
 
-    def whole2(lo, hi):
-        do("S", lambda e: e.activation(T.rn[:, lo:hi], T.tm[:, lo:hi], Fn.Copy, bias=-MAGIC), [("tm", lo, hi)], [("rn", lo, hi)])
+    def whole2(k, j0, j1):
+        j, n = 512 * k + j0, j1 - j0
+        do("S", lambda e: e.activation(T.rn[:, j:j + n], T.tm[:, j:j + n], Fn.Copy, bias=-MAGIC), [("tm", j, j + n)], [("rn", j, j + n)])
 
     def frac(s, k):
         for h in range(2):
-            a, at, p = 2 * k + h, 512 * s + 256 * k + 128 * h, 512 * (4 + k) + RUNS[s][h]
-            do("V", lambda v: v.tensor_tensor(T.fr[:, 2048 * s + 4 * a:2048 * s + 2048:16], T.ps[:, p:p + 128], T.rn[:, at:at + 128], Op.subtract),
-               bank(4 + k) + [("rn", at, at + 128)], [("fr0%d" % a, 512 * s, 512 * s + 512)])
+            a, j, n = 2 * k + h, 512 * k + RUNS[s][h], WIDE[s]
+            do("V", lambda v: v.tensor_tensor(T.fr[:, 4 * AT[s] + 4 * a:4 * AT[s + 1]:16], T.ps[:, 2048 + j:2048 + j + n], T.rn[:, j:j + n], Op.subtract),
+               bank(4 + k) + [("rn", j, j + n)], [("fr0%d" % a, AT[s], AT[s + 1])])
 
     def spread(q, lo, hi, bs):
         for b in bs:
             copy(q, T.fr[:, 4 * lo + b:4 * hi:4], T.fr[:, 4 * lo:4 * hi:4], each("fr0", lo, hi), [("fr%d" % b, lo, hi)])
 
-    def inside(s):
-        at = (128 * s, 128 * s + 128)
-        ab, sg = T.ab[:, at[0]:at[1]], T.sg[:, at[0]:at[1]]
-        return [lambda: do("S", lambda e: e.activation(ab, T.ps[:, 512 * (6 + s):512 * (6 + s) + 128], Fn.Abs), bank(6 + s), [("ab", *at)]),
-                lambda: do("S", lambda e: e.activation(sg, ab, Fn.Sign, bias=float(CL), scale=-1.0), [("ab", *at)], [("sg", *at)])]
+    def rounded(s):
+        lo, hi = AT[s] // 4, AT[s + 1] // 4
+        d = T.ps[:, 512 * LB[s] + skip(s):512 * LB[s] + skip(s) + hi - lo]
+        return [lambda: do("S", lambda e: e.activation(T.ab[:, lo:hi], d, Fn.Abs), bank(LB[s]), [("ab", lo, hi)]),
+                lambda: do("V", lambda v: v.tensor_scalar(T.ni[:, lo:hi], d, float(-CL), float(CL), Op.max, Op.min), bank(LB[s]), [("ni", lo, hi)])]
 
-    def lists(s):
-        lo, hi = 128 * s, 128 * s + 128
-        ni, pl, sg, dp, vl, dl, bas = (T[n][:, lo:hi] for n in ("ni", "pl", "sg", "dp", "vl", "dl", "bas"))
+    def lists(lo, hi):
+        ni, pl, ab, sg, dp, vl, dl, bas = (T[n][:, lo:hi] for n in ("ni", "pl", "ab", "sg", "dp", "vl", "dl", "bas"))
         key = lambda *n: [(m, lo, hi) for m in n]
-        d, b = T.ps[:, 512 * (6 + s):512 * (6 + s) + 128], T.pflt[:, 0:1]
+        col = 2 + (lo > 0)
+        add = T.pflt[:, col:col + 1]
 
         def place():
             do("V", lambda v: v.tensor_tensor(pl, ni, bas, Op.add), key("ni", "bas"), key("pl"))
-            if s == E and prev is None:
-                do("V", lambda v: v.tensor_scalar(pl, pl, float(OWN - first[s]), None, Op.max), key("pl"), key("pl"))
-            if s == E and nxt is None:
-                do("V", lambda v: v.tensor_scalar(pl, pl, float(RGT - 1 - first[s]), None, Op.min), key("pl"), key("pl"))
+            if lo > 0 and None in (prev, nxt):
+                part = T.pl[:, 128:192] if prev is None else T.pl[:, 192:256]
+                do("V", lambda v: v.tensor_scalar(part, part, T.pflt[:, 4:5], None, Op.max if prev is None else Op.min),
+                   key("pl") + [("pflt", 4, 5)], key("pl"))
         return [
-            lambda: do("V", lambda v: v.tensor_scalar(ni, d, float(-CL), float(CL), Op.max, Op.min), bank(6 + s), key("ni")),
+            lambda: do("S", lambda e: e.activation(sg, ab, Fn.Sign, bias=float(CL), scale=-1.0), key("ab"), key("sg")),
             place,
-            lambda: do("V", lambda v: v.tensor_scalar(vl, pl, 4.0, b, Op.mult, Op.add), key("pl") + [("pflt", 0, 1)], key("vl")),
+            lambda: do("V", lambda v: v.tensor_scalar(vl, pl, 4.0, add, Op.mult, Op.add), key("pl") + [("pflt", col, col + 1)], key("vl")),
             lambda: do("V", lambda v: v.tensor_tensor(dp, pl, sg, Op.mult), key("pl", "sg"), key("dp")),
-            lambda: do("V", lambda v: v.tensor_scalar(dl, dp, 4.0, b, Op.mult, Op.add), key("dp") + [("pflt", 0, 1)], key("dl"))]
+            lambda: do("V", lambda v: v.tensor_scalar(dl, dp, 4.0, add, Op.mult, Op.add), key("dp") + [("pflt", col, col + 1)], key("dl"))]
+
+    set_of = lambda lo: max(s for s in (A, LO, HI) if AT[s] <= lo)
 
     def window(name, lo, hi):
-        s = lo // 512
-        last = end[s] - (name == "dw" and (s == A or nxt is not None))
+        s = set_of(lo)
+        last = end[s] - (name == "dw" and (s != HI or nxt is not None))
         lst = "dl" if name == "dw" else "vl"
-        return T[name][:, 4 * first[s]:4 * last].indirect(T[lst][:, lo // 4:hi // 4]), each(name, first[s], last) + [(lst, 128 * s, 128 * s + 128)]
+        return T[name][:, 4 * first[s]:4 * last].indirect(T[lst][:, lo // 4:hi // 4]), each(name, first[s], last) + [(lst, lo // 4, hi // 4)]
 
     def slope(lo, hi):
         win, reads = window("dw", lo, hi)
@@ -300,10 +307,11 @@ def rank_program(g, core, T, topo):
     def products(lo, hi, banks):
         for o in range(2):
             for k in range(2):
-                mm(banks[o], hi - lo - 2, "wq", 128 * (2 * k + o), "mq", lo + 2 * k, k == 0, k == 1)
+                mm(banks[o], max(hi - lo - 2, 128), "wq", 128 * (2 * k + o), "mq", lo + 2 * k, k == 0, k == 1)
 
     def to_y(lo, hi, banks, qs, blocks=(0, 1)):
-        s, c0, n = lo // 512, lo % 512 // 4, (hi - lo) // 4
+        s = set_of(lo)
+        c0, n = (lo - AT[s]) // 4, (hi - lo) // 4
         for o in blocks:
             for h in range(2):
                 j = TC * o + RUNS[s][h] + c0
@@ -320,23 +328,24 @@ def rank_program(g, core, T, topo):
         for b in range(4):
             mm(b, h1 - h0, "eq", 128 * b, "hq", h0, True, True)
 
-    def hc(b, q="SS"):
+    def cl(b, q="S"):
         if prev is not None:
-            unpack_copy(b, 0, 0, HAL, q[0])
-        if nxt is not None:
-            unpack_copy(b, HAL - h0, RGT, HAL, q[1])
+            unpack_copy(b, 0, 0, HAL, q)
 
-    def hd(b):
+    def cr(b, q="S"):
+        if nxt is not None:
+            unpack_copy(b, HAL - h0, RGT, HAL, q)
+
+    def dl(b):
         if prev is not None:
             diff(b, 0, 0, 1, HAL - 1)
+
+    def dr(b):
         if nxt is not None:
             diff(b, HAL - h0, RGT, RGT - 1, WIN - 1)
 
-    def halo(b):
-        hc(b); hd(b)
-
-    def quant_x(half):
-        quant("xq", "xs", "xt", 256 * half, 256, 1024 * half, 256 * half, 256 * half + 256)
+    def quant_x(i):
+        quant("xq", "xs", "xt", 128 * i, 128, 512 * i, 128 * i, 128 * i + 128)
 
     def quant_w():
         quant("wq", "ws", "wt", 0, 512, 0, 0, 1)
@@ -349,8 +358,17 @@ def rank_program(g, core, T, topo):
     c1 = lambda b, q="S": unpack_copy(b, 0, OWN, 256, q)
     d1 = lambda b: diff(b, 0, OWN, OWN + 1, OWN + 255)
     c2 = lambda b, q="S": unpack_copy(b, 0, H2, 256, q)
+    c3 = lambda b, q="S": unpack_copy(b, 256, H2, 256, q)
+    d3 = lambda b: diff(b, 0, OWN, OWN + 1, RGT - 1)
+
+    def unpack_all(b):
+        mm(b, 512, "eq", 128 * b, "xq", 0, True, True)
+
+    def dbl(q, w):
+        copy(q, T.zo[:, :, w:2 * w], T.zo[:, :, 0:w], [("zo", 0, w // 4)], [("zo", w // 4, w // 2)])
+
     d2 = lambda b: diff(b, 0, H2, H2 - 1, RGT - 1)
-    la, ia, le, ie = lists(A), inside(A), lists(E), inside(E)
+    ra, rl, rh, la, le = rounded(A), rounded(LO), rounded(HI), lists(0, 128), lists(128, 256)
 
     def load_w():
         after("Y", [("xt", 0, 512)], [])
@@ -363,46 +381,50 @@ def rank_program(g, core, T, topo):
         for b in bs:
             mm(b, 256, "eq", 128 * b, "xq", 256 * half, True, True)
 
-    quant_e(1); quant_e(2); quant_e(3); base(A); base(E)
-    four("V", 0); four("V", 1); four("V", 2); four("S", 3); sixteen("S", 1); sixteen("S", 2)
+    quant_e(1); quant_e(2); quant_e(3)
+    four("V", 0); four("V", 1); four("V", 2); four("S", 3); shift(A); shift(LO); sixteen("S", 1); sixteen("S", 2)
+    quant_x(0); quant_x(3); sent = send()
+    quant_x(1); unpack_mm(0)
     among("V", 0); among("V", 1)
-    quant_x(0); unpack_mm(0)
     sixteen("V", 3); quant_zl()
-    quant_x(1); sent = send(); load_w()
-    quant_zo(); list_mm(A); list_mm(E); offs_mm(0); offs_mm(1)
+    quant_x(2); load_w()
+    quant_zo(); list_mm(A); offs_mm(0); offs_mm(1)
     for b in range(4):
         c1(b); d1(b)
-    unpack_mm(1)
+    ra[0](); ra[1]()
+    unpack_mm(1, (0, 1)); list_mm(LO); list_mm(HI); unpack_mm(1, (2, 3))
 
-    ia[0](); la[0](); ie[0](); whole("S", A, 0); ia[1](); whole2(0, 256)
-    whole("V", A, 1); la[1](); le[0](); la[2](); frac(A, 1); la[3](); frac(A, 0); la[4]()
-    c2(0); c2(1); c2(2); c2(3)
-    whole("V", E, 0); whole("V", E, 1)
-    spread("S", 0, 256, (1, 2, 3)); spread("G", 256, 512, (2, 3)); spread("S", 256, 512, (1,))
-    d2(0); d2(1); frac(E, 0); frac(E, 1); d2(2); d2(3)
+    whole("S", 0, 0, TC); la[0](); whole2(0, 0, TC)
+    la[1](); whole("V", 1, 0, TC); la[2](); frac(A, 1); la[3](); frac(LO, 1); frac(A, 0); la[4]()
+    c2(0); c2(1); rl[0](); rh[0](); c2(2); c2(3)
+    spread("G", 0, 256, (1,)); spread("S", 0, 256, (2, 3)); spread("G", 256, 512, (1, 2, 3)); le[0]()
+    frac(LO, 0); d2(0); rl[1](); rh[1](); d2(1); le[1](); d2(2); frac(HI, 1); frac(HI, 0); d2(3)
+    spread("G", 512, 768, (1, 2))
 
-    slope(0, 256); ie[1](); far_v(0, 256)
-    spread("G", 512, 768, (1, 2)); far_add(0, 256)
-    slope(256, 512); far_v(256, 512)
-    spread("G", 512, 768, (3,)); far_add(256, 512); spread("G", 768, 1024, (1, 2, 3))
-    halo_mm()
-    le[1](); quant_w(); le[2](); le[3]()
-    halo(0); le[4](); halo(1); halo(2); halo(3); seam()
+    slope(0, 256); far_v(0, 256); far_add(0, 256)
+    le[3](); le[2](); slope(256, 512); far_v(256, 512); far_add(256, 512)
+    halo_mm(); le[4]()
+    for b in range(4):
+        cl(b); dl(b)
+    seam(); spread("S", 512, 768, (3,)); spread("G", 768, 1024, (1, 2))
 
-    P1, P2 = 752, 888
-    c = (P1 - TC) // 4
-    slope(TC, P1); far_v(TC, P1); far_add(TC, P1)
-    slope(P1, P2); far_v(P1, P2); far_add(P1, P2)
-    quant_m(0, TC); products(0, TC, (4, 5))
-    slope(P2, 2 * TC)
+    slope(512, 768); far_v(512, 768); far_add(512, 768)
+    quant_w()
+    for b in range(4):
+        cr(b); dr(b)
+    spread("S", 768, 1024, (3,))
+    P = 888
+    slope(768, P); far_v(768, P); far_add(768, P)
+    quant_m(0, 512); products(0, 512, (4, 5))
+    slope(P, 1024)
     for o in range(2):
-        to_y(0, TC, (4, 5), "SSSS", (o,)); store("Y", TC * o + 128, TC * o + 384)
-    quant_m(TC, P1); products(TC, P1, (6, 7))
-    tap(P2, 2 * TC)
+        to_y(0, 512, (4, 5), "SSSS", (o,)); store("Y", TC * o + 128, TC * o + 384)
+    quant_m(512, 768); products(512, 768, (6, 7))
+    tap(P, 1024)
     for o in range(2):
-        to_y(TC, P1, (6, 7), "SSSS", (o,)); store("Y", TC * o, TC * o + c); store("Y", TC * o + 384, TC * o + 384 + c)
-    quant_m(P1, 2 * TC); products(P1, 2 * TC, (2, 3))
+        to_y(512, 768, (6, 7), "SSSS", (o,)); store("Y", TC * o, TC * o + 128)
+    quant_m(768, 1024); products(768, 1024, (2, 3))
     for o in range(2):
-        to_y(P1, 2 * TC, (2, 3), "VVVV", (o,)); store("Y", TC * o + c, TC * o + 128); store("S", TC * o + 384 + c, TC * o + TC)
+        to_y(768, 1024, (2, 3), "VVVV", (o,)); store("YS"[o], TC * o + 384, TC * o + TC)
     g.wait_ge(T.sem.sent, sent)
     drain("Y")

from concourse.bass import DstId, RemoteDMATransfer
from concourse.mybir import dt, AluOpType, ActivationFunctionType

N, TC, CL = 4, 512, 127
HAL = 128
OWN, RGT, WIN = 128, 640, 768
MAGIC = 12582912.0
A, LO, HI = 0, 1, 2
RUNS = ((128, 256), (0, 64), (384, 448))
WIDE = (128, 64, 64)
AT = (0, 512, 768, 1024)

F32, BF, F16, U16, I32 = "float32", "bfloat16", "float16", "uint16", "int32"
X4 = "float8_e4m3fn_x4"
SCRATCH = {
    "xt": ("sbuf", [128, 4 * TC], BF),
    "us": ("sbuf", [128, 16, 4], BF),
    "zo": ("sbuf", [128, 16, 64], BF),
    "zl": ("sbuf", [128, 9, 64], BF),
    "wt": ("sbuf", [128, 4 * TC], BF),
    "ones": ("sbuf", [128, 128], BF),
    "unit": ("sbuf", [128, 528], BF),
    "pidx": ("sbuf", [128, 2], I32),
    "pint": ("sbuf", [128, 4], I32),
    "pflt": ("sbuf", [128, 8], F32),
    "xq": ("sbuf", [128, TC], X4), "xs": ("sbuf", [128, TC], "uint8"),
    "zq": ("sbuf", [128, 400], X4), "zs": ("sbuf", [128, 400], "uint8"),
    "eq": ("sbuf", [128, 512], X4), "es": ("sbuf", [128, 512], "uint8"),
    "wq": ("sbuf", [128, 512], X4), "ws": ("sbuf", [128, 512], "uint8"),
    "hq": ("sbuf", [128, 2 * HAL], X4), "hs": ("sbuf", [128, 2 * HAL], "uint8"),
    "mq": ("sbuf", [128, 2 * TC + 2], X4), "ms": ("sbuf", [128, 2 * TC + 2], "uint8"),
    "vw": ("sbuf", [128, 4 * WIN], F32), "dw": ("sbuf", [128, 4 * WIN], F32),
    "tm": ("sbuf", [128, 2 * TC], F32), "rn": ("sbuf", [128, 2 * TC], F32),
    "fr": ("sbuf", [128, 8 * TC], F32), "pp": ("sbuf", [128, 8 * TC], F32), "mt": ("sbuf", [128, 8 * TC + 8], BF),
    "bas": ("sbuf", [128, 256], I32), "ni": ("sbuf", [128, 256], I32), "pl": ("sbuf", [128, 256], F16),
    "dp": ("sbuf", [128, 256], F16), "ab": ("sbuf", [128, 256], F32), "sg": ("sbuf", [128, 256], F32),
    "vl": ("sbuf", [128, 256], U16), "dl": ("sbuf", [128, 256], U16),
    "yb": ("sbuf", [128, 2 * TC], F32),
    "ps": ("psum", [128, 4096], F32),
}
SEMAPHORES = ["cV", "cS", "cP", "cG", "sent", "arrR", "arrL", "dx0", "dx1", "dx2", "dx3", "du", "dwt"] + \
    ["dy%d" % i for i in range(12)] + ["da%d" % i for i in range(6)]

Op, Fn = AluOpType, ActivationFunctionType


def scheduler(g, T):
    queues = {"V": g.vector, "S": g.scalar, "P": g.tensor, "G": g, "Y": g.sync}
    clock = {q: {} for q in queues}
    done = {}
    tick, log, scale = {}, {}, {}

    def after(q, reads, writes):
        deps = {}
        for acc, mine in ((reads, "r"), (writes, "w")):
            for key, lo, hi in acc:
                for (l, h, kind, src, t, oq) in log.get(key, []):
                    if h <= lo or hi <= l:
                        continue
                    bank = key[:2] == "ps"
                    if mine == "r" and kind == "r" and not (bank and oq != q):
                        continue
                    if src == "c" + q and bank:
                        continue
                    deps[src] = max(deps.get(src, 0), t)
        for src, t in list(deps.items()):
            if clock[q].get(src, 0) >= t:
                continue
            if any(s2 != src and done[(s2, t2)].get(src, 0) >= t and clock[q].get(s2, 0) < t2 for s2, t2 in deps.items()):
                continue
            queues[q].wait_ge(T.sem[src], t * scale.get(src, 1))
        for src, t in deps.items():
            for s, v in done[(src, t)].items():
                clock[q][s] = max(clock[q].get(s, 0), v)

    def note(q, src, reads, writes):
        tick[src] = tick.get(src, 0) + 1
        c = dict(clock[q]) if q else {}
        c[src] = tick[src]
        done[(src, tick[src])] = c
        for acc, kind in ((reads, "r"), (writes, "w")):
            for key, lo, hi in acc:
                log.setdefault(key, []).append((lo, hi, kind, src, tick[src], q))

    def do(q, call, reads, writes):
        after(q, reads, writes)
        call(queues[q]).then_inc(T.sem["c" + q], 1)
        note(q, "c" + q, reads, writes)

    def dma(q, sem, out, in_, reads, writes, **kw):
        after(q, reads, writes)
        queues[q].dma_start(out, in_, **kw).then_inc(T.sem[sem], 16)
        scale[sem] = 16
        note(q, sem, reads, writes)

    def arrival(sem, count, writes):
        scale[sem] = count
        note(None, sem, [], writes)

    def drain(q):
        for src, t in tick.items():
            if clock[q].get(src, 0) < t:
                queues[q].wait_ge(T.sem[src], t * scale.get(src, 1))

    return do, dma, after, arrival, drain


def rank_program(g, core, T, topo):
    rank = T.rank_of(core)
    if rank is None:
        return
    do, dma, after, arrival, drain = scheduler(g, T)
    prev = T.cores[rank - 1] if rank > 0 else None
    nxt = T.cores[rank + 1] if rank < N - 1 else None
    ENG = 4
    if prev is not None:
        arrival("arrL", 2 * ENG, [("hq", 0, HAL)])
    if nxt is not None:
        arrival("arrR", 2 * ENG, [("hq", HAL, 2 * HAL)])
    first = (OWN,) + 2 * (0 if prev is not None else OWN - 2,)
    end = (RGT, RGT, WIN if nxt is not None else RGT)
    each = lambda name, lo, hi, bs=range(4): [("%s%d" % (name, b), lo, hi) for b in bs]
    bank = lambda n: [("ps%d" % n, 0, 512)]

    def quant(codes, planes, buf, c0, n, e0, lo, hi):
        do("V", lambda v: v.quantize_mx(T[codes][:, c0:c0 + n], T[planes][:, c0:c0 + n], T[buf][:, e0:e0 + 4 * n]),
           [(buf, lo, hi)], [(codes, c0, c0 + n)])

    names = {"zq": "zs", "xq": "xs", "eq": "es", "wq": "ws", "hq": "hs", "mq": "ms"}

    def mm(n, cols, ls, l0, rs, r0, start, stop):
        do("P", lambda p: p.matmul_mx(T.ps[:, 512 * n:512 * n + cols], T[ls][:, l0:l0 + 128], T[names[ls]][:, l0:l0 + 128],
                                      T[rs][:, r0:r0 + cols], T[names[rs]][:, r0:r0 + cols], start, stop),
           [(ls, l0, l0 + 128), (rs, r0, r0 + cols)], bank(n))

    def copy(q, out, in_, reads, writes):
        if q == "G":
            do(q, lambda e: e.affine_select(out, in_, [[1, n] for n in out.shape[1:]], Op.is_gt, 0.0, 1, 0), reads, writes)
        else:
            do(q, lambda e: e.activation(out, in_, Fn.Copy) if q == "S" else e.tensor_copy(out, in_), reads, writes)

    dma("S", "du", T.us[:, :, :], T.u[:, 0:64], [], [("us", 0, 1)])
    for q, i in (("Y", 0), ("S", 3), ("Y", 1), ("S", 2)):
        dma(q, "dx%d" % i, T.xt[:, 512 * i:512 * i + 512], T.x[:, 512 * i:512 * i + 512], [], [("xt", 128 * i, 128 * i + 128)])

    do("G", lambda e: e.iota(T.pidx[:, 0:1], [[0, 1]], 0, 1), [], [("pidx", 0, 1)])
    do("G", lambda e: e.iota(T.bas[:, 0:128], [[1, 128]], OWN + RUNS[A][0] - first[A] + 4 * WIDE[A] + 1, 0), [], [("bas", 0, 128)])
    do("V", lambda v: v.memset(T.ones[:], 1.0), [], [("ones", 0, 1)])
    do("V", lambda v: v.memset(T.unit[:], 0.0), [], [("unit", 0, 1)])
    do("G", lambda e: e.affine_select(T.unit[:, 3:515:4], T.ones[:], [[-1, 128]], Op.is_equal, 0.0, 0, 1),
       [("ones", 0, 1)], [("unit", 0, 1)])
    do("V", lambda v: v.memset(T.zl[:, :, :], 0.0), [], [("zl", 0, 2)])
    do("G", lambda e: e.iota(T.bas[:, 128:256], [[RUNS[HI][0], 2], [1, 64]], OWN - first[LO] + 4 * WIDE[LO] + 1, 0), [], [("bas", 128, 256)])
    zeros = [("dw", OWN, OWN + 1), ("dw", first[LO], first[LO] + 1)]
    if prev is None:
        zeros = [("dw", OWN - 2, OWN + 1), ("vw", OWN - 2, OWN)]
    if nxt is None:
        zeros.append(("dw", RGT - 1, RGT))
    for w, lo, hi in zeros:
        do("G", lambda e: e.iota(T[w][:, 4 * lo:4 * hi], [[0, 4 * (hi - lo)]], 0, 0, allow_small_or_imprecise_dtypes=True), [], each(w, lo, hi))
    do("V", lambda v: v.tensor_scalar(T.pint[:, 0:1], T.pidx[:, 0:1], 3, None, Op.bitwise_and), [("pidx", 0, 1)], [("pint", 0, 1)])
    do("V", lambda v: v.tensor_scalar(T.pint[:, 1:2], T.pidx[:, 0:1], 2, 1, Op.arith_shift_right, Op.bitwise_and),
       [("pidx", 0, 1)], [("pint", 1, 2)])

    def quant_e(b):
        quant("eq", "es", "unit", 128 * b, 128, 3 - b, 0, 1)

    quant_e(0)
    do("V", lambda v: v.tensor_scalar(T.pflt[:, 0:2], T.pint[:, 0:2], -4.0, None, Op.add), [("pint", 0, 2)], [("pflt", 0, 1)])

    def shift(s):
        do("S", lambda e: e.activation(T.pflt[:, 2 + s:3 + s], T.pflt[:, 1:2], Fn.Identity, bias=T.pflt[:, 0:1], scale=4.0 * WIDE[s]),
           [("pflt", 0, 1)], [("pflt", 2 + s, 3 + s)])
        if s == LO and None in (prev, nxt):
            edge = OWN - first[LO] + 1 if prev is None else RGT - first[HI]
            do("S", lambda e: e.activation(T.pflt[:, 4:5], T.pflt[:, 1:2], Fn.Copy, bias=float(edge), scale=-float(WIDE[s])),
               [("pflt", 0, 1)], [("pflt", 4, 5)])

    def four(q, r):
        copy(q, T.zo[:, :, 4 * r:4 * r + 4], T.us[:, :, :], [("us", 0, 1)], [("zo", r, r + 1)])

    def among(q, k):
        copy(q, T.zl[:, 0:8, 32 * k + 16:32 * k + 32], T.zo[:, 8 * k:8 * k + 8, 0:16], [("zo", 0, 4)], [("zl", k, k + 1)])

    def sixteen(q, r):
        copy(q, T.zo[:, :, 16 * r:16 * r + 16], T.zo[:, :, 0:16], [("zo", 0, 4)], [("zo", 4 * r, 4 * r + 4)])

    def quant_zl():
        do("V", lambda v: v.quantize_mx(T.zq[:, 0:144], T.zs[:, 0:144], T.zl[:, :, :]), [("zl", 0, 2)], [("zq", 0, 144)])

    def quant_zo():
        do("V", lambda v: v.quantize_mx(T.zq[:, 144:400], T.zs[:, 144:400], T.zo[:, :, :]), [("zo", 0, 16)], [("zq", 144, 400)])

    def send():
        sends = []
        if prev is not None:
            sends.append((prev, 0, HAL, "arrR"))
        if nxt is not None:
            sends.append((nxt, TC - HAL, 0, "arrL"))
        after("G", [("xq", c0, c0 + HAL) for _, c0, _, _ in sends], [])
        for plane in (0, 1):
            tr = []
            for i, (dst, c0, d0, sem) in enumerate(sends):
                rid, pid, _ = topo.addr(dst)
                eng = topo.engines(core, dst)[ENG * i:ENG * i + ENG]
                s, d = (T.xs[:, c0:c0 + HAL], T.hs[:, d0:d0 + HAL]) if plane else \
                    (T.xq[:, c0:c0 + HAL].bitcast(dt.uint8), T.hq[:, d0:d0 + HAL].bitcast(dt.uint8))
                tr.append(RemoteDMATransfer(dst_ids=[DstId(rid=rid, pnc=pid)], dma_engine_mask=sum(1 << e for e in eng),
                                            remote_sem=T.sem[sem], src=s, dst=d))
            g.remote_dma_fused(tr, local_sem=T.sem.sent)
        return 2 * ENG * len(sends)

    def unpack_copy(b, p0, w0, n, q="S"):
        copy(q, T.vw[:, 4 * w0 + b:4 * (w0 + n):4], T.ps[:, 512 * b + p0:512 * b + p0 + n], bank(b), [("vw%d" % b, w0, w0 + n)])

    def diff(b, p0, w0, lo, hi):
        p = 512 * b + p0 - w0 + 1
        do("V", lambda v: v.tensor_tensor(T.dw[:, 4 * lo + b:4 * hi:4], T.ps[:, p + lo:p + hi], T.vw[:, 4 * lo + b:4 * hi:4], Op.subtract),
           bank(b) + [("vw%d" % b, lo, hi)], [("dw%d" % b, lo, hi)])

    LB = (6, 7, 6)
    skip = lambda s: 128 - WIDE[s] if s == HI else 0

    def list_mm(s):
        for h in range(2):
            mm(LB[s], 128, "zq", 4 - 4 * h, "xq", RUNS[s][h] - skip(s), h == 0, h == 1)

    def whole(q, k, j0, j1):
        j, n = 512 * k + j0, j1 - j0
        d = T.ps[:, 2048 + j:2048 + j + n]
        if q == "V":
            do(q, lambda v: v.tensor_scalar(T.rn[:, j:j + n], d, MAGIC, -MAGIC, Op.add, Op.add), bank(4 + k), [("rn", j, j + n)])
        else:
            do(q, lambda e: e.activation(T.tm[:, j:j + n], d, Fn.Copy, bias=MAGIC), bank(4 + k), [("tm", j, j + n)])

    def whole2(k, j0, j1):
        j, n = 512 * k + j0, j1 - j0
        do("S", lambda e: e.activation(T.rn[:, j:j + n], T.tm[:, j:j + n], Fn.Copy, bias=-MAGIC), [("tm", j, j + n)], [("rn", j, j + n)])

    def frac(s, k):
        for h in range(2):
            a, j, n = 2 * k + h, 512 * k + RUNS[s][h], WIDE[s]
            do("V", lambda v: v.tensor_tensor(T.fr[:, 4 * AT[s] + 4 * a:4 * AT[s + 1]:16], T.ps[:, 2048 + j:2048 + j + n], T.rn[:, j:j + n], Op.subtract),
               bank(4 + k) + [("rn", j, j + n)], [("fr0%d" % a, AT[s], AT[s + 1])])

    def spread(q, lo, hi, bs):
        for b in bs:
            copy(q, T.fr[:, 4 * lo + b:4 * hi:4], T.fr[:, 4 * lo:4 * hi:4], each("fr0", lo, hi), [("fr%d" % b, lo, hi)])

    def rounded(s):
        lo, hi = AT[s] // 4, AT[s + 1] // 4
        d = T.ps[:, 512 * LB[s] + skip(s):512 * LB[s] + skip(s) + hi - lo]
        return [lambda: do("S", lambda e: e.activation(T.ab[:, lo:hi], d, Fn.Abs), bank(LB[s]), [("ab", lo, hi)]),
                lambda: do("V", lambda v: v.tensor_scalar(T.ni[:, lo:hi], d, float(-CL), float(CL), Op.max, Op.min), bank(LB[s]), [("ni", lo, hi)])]

    def lists(lo, hi):
        ni, pl, ab, sg, dp, vl, dl, bas = (T[n][:, lo:hi] for n in ("ni", "pl", "ab", "sg", "dp", "vl", "dl", "bas"))
        key = lambda *n: [(m, lo, hi) for m in n]
        col = 2 + (lo > 0)
        add = T.pflt[:, col:col + 1]

        def place():
            do("V", lambda v: v.tensor_tensor(pl, ni, bas, Op.add), key("ni", "bas"), key("pl"))
            if lo > 0 and None in (prev, nxt):
                part = T.pl[:, 128:192] if prev is None else T.pl[:, 192:256]
                do("V", lambda v: v.tensor_scalar(part, part, T.pflt[:, 4:5], None, Op.max if prev is None else Op.min),
                   key("pl") + [("pflt", 4, 5)], key("pl"))
        return [
            lambda: do("S", lambda e: e.activation(sg, ab, Fn.Sign, bias=float(CL), scale=-1.0), key("ab"), key("sg")),
            place,
            lambda: do("V", lambda v: v.tensor_scalar(vl, pl, 4.0, add, Op.mult, Op.add), key("pl") + [("pflt", col, col + 1)], key("vl")),
            lambda: do("V", lambda v: v.tensor_tensor(dp, pl, sg, Op.mult), key("pl", "sg"), key("dp")),
            lambda: do("V", lambda v: v.tensor_scalar(dl, dp, 4.0, add, Op.mult, Op.add), key("dp") + [("pflt", col, col + 1)], key("dl"))]

    set_of = lambda lo: max(s for s in (A, LO, HI) if AT[s] <= lo)

    def window(name, lo, hi):
        s = set_of(lo)
        last = end[s] - (name == "dw" and (s != HI or nxt is not None))
        lst = "dl" if name == "dw" else "vl"
        return T[name][:, 4 * first[s]:4 * last].indirect(T[lst][:, lo // 4:hi // 4]), each(name, first[s], last) + [(lst, lo // 4, hi // 4)]

    def slope(lo, hi):
        win, reads = window("dw", lo, hi)
        do("V", lambda v: v.tensor_tensor(T.pp[:, 4 * lo:4 * hi], win, T.fr[:, 4 * lo:4 * hi], Op.mult),
           reads + each("fr0", lo, hi) + each("fr", lo, hi, (1, 2, 3)), [("pp", lo, hi)])

    def tap(lo, hi):
        win, reads = window("vw", lo, hi)
        do("V", lambda v: v.tensor_tensor(T.mt[:, 4 * lo:4 * hi], win, T.pp[:, 4 * lo:4 * hi], Op.add), reads + [("pp", lo, hi)], [("mt", lo, hi)])

    def far_v(lo, hi):
        win, reads = window("vw", lo, hi)
        do("S", lambda e: e.activation(T.mt[:, 4 * lo:4 * hi], win, Fn.Copy), reads, [("mt", lo, hi)])

    adds = [0]

    def far_add(lo, hi):
        dma("G", "da%d" % adds[0], T.mt[:, 4 * lo:4 * hi], T.pp[:, 4 * lo:4 * hi], [("pp", lo, hi), ("mt", lo, hi)], [("mt", lo, hi)], accum_op=Op.add)
        adds[0] += 1

    def quant_m(lo, hi):
        quant("mq", "ms", "mt", lo, hi - lo, 4 * lo, lo, hi)

    stores = [0]

    def products(lo, hi, banks):
        for o in range(2):
            for k in range(2):
                mm(banks[o], max(hi - lo - 2, 128), "wq", 128 * (2 * k + o), "mq", lo + 2 * k, k == 0, k == 1)

    def to_y(lo, hi, banks, qs, blocks=(0, 1)):
        s = set_of(lo)
        c0, n = (lo - AT[s]) // 4, (hi - lo) // 4
        for o in blocks:
            for h in range(2):
                j = TC * o + RUNS[s][h] + c0
                copy(qs[2 * o + h], T.yb[:, j:j + n], T.ps[:, 512 * banks[o] + h:512 * banks[o] + 4 * n - 2:4], bank(banks[o]), [("yb", j, j + n)])

    def store(q, j0, j1):
        dma(q, "dy%d" % stores[0], T.y[:, j0:j1], T.yb[:, j0:j1], [("yb", j0, j1)], [])
        stores[0] += 1

    H2 = OWN + 256
    h0, h1 = (0 if prev is not None else HAL), (2 * HAL if nxt is not None else HAL)

    def halo_mm():
        for b in range(4):
            mm(b, h1 - h0, "eq", 128 * b, "hq", h0, True, True)

    def cl(b, q="S"):
        if prev is not None:
            unpack_copy(b, 0, 0, HAL, q)

    def cr(b, q="S"):
        if nxt is not None:
            unpack_copy(b, HAL - h0, RGT, HAL, q)

    def dl(b):
        if prev is not None:
            diff(b, 0, 0, 1, HAL - 1)

    def dr(b):
        if nxt is not None:
            diff(b, HAL - h0, RGT, RGT - 1, WIN - 1)

    def quant_x(i):
        quant("xq", "xs", "xt", 128 * i, 128, 512 * i, 128 * i, 128 * i + 128)

    def quant_w():
        quant("wq", "ws", "wt", 0, 512, 0, 0, 1)

    def seam():
        lo = OWN - 1 if prev is not None else OWN
        do("V", lambda v: v.tensor_tensor(T.dw[:, 4 * lo:4 * OWN + 4], T.vw[:, 4 * lo + 4:4 * OWN + 8], T.vw[:, 4 * lo:4 * OWN + 4], Op.subtract),
           each("vw", lo, OWN + 2), each("dw", lo, OWN + 1))

    c1 = lambda b, q="S": unpack_copy(b, 0, OWN, 256, q)
    d1 = lambda b: diff(b, 0, OWN, OWN + 1, OWN + 255)
    c2 = lambda b, q="S": unpack_copy(b, 0, H2, 256, q)
    c3 = lambda b, q="S": unpack_copy(b, 256, H2, 256, q)
    d3 = lambda b: diff(b, 0, OWN, OWN + 1, RGT - 1)

    def unpack_all(b):
        mm(b, 512, "eq", 128 * b, "xq", 0, True, True)

    def dbl(q, w):
        copy(q, T.zo[:, :, w:2 * w], T.zo[:, :, 0:w], [("zo", 0, w // 4)], [("zo", w // 4, w // 2)])

    d2 = lambda b: diff(b, 0, H2, H2 - 1, RGT - 1)
    ra, rl, rh, la, le = rounded(A), rounded(LO), rounded(HI), lists(0, 128), lists(128, 256)

    def load_w():
        after("Y", [("xt", 0, 512)], [])
        dma("Y", "dwt", T.wt[:], T.w[:], [], [("wt", 0, 1)])

    def offs_mm(k):
        mm(4 + k, TC, "zq", 144 + 128 * k, "xq", 0, True, True)

    def unpack_mm(half, bs=range(4)):
        for b in bs:
            mm(b, 256, "eq", 128 * b, "xq", 256 * half, True, True)

    quant_e(1); quant_e(2); quant_e(3)
    four("V", 0); four("V", 1); four("V", 2); four("S", 3); shift(A); shift(LO); sixteen("S", 1); sixteen("S", 2)
    quant_x(0); quant_x(3); sent = send()
    quant_x(1); unpack_mm(0)
    among("V", 0); among("V", 1)
    sixteen("V", 3); quant_zl()
    quant_x(2); load_w()
    quant_zo(); list_mm(A); offs_mm(0); offs_mm(1)
    for b in range(4):
        c1(b); d1(b)
    ra[0](); ra[1]()
    unpack_mm(1, (0, 1)); list_mm(LO); list_mm(HI); unpack_mm(1, (2, 3))

    whole("S", 0, 0, TC); la[0](); whole2(0, 0, TC)
    la[1](); whole("V", 1, 0, TC); la[2](); frac(A, 1); la[3](); frac(LO, 1); frac(A, 0); la[4]()
    c2(0); c2(1); rl[0](); rh[0](); c2(2); c2(3)
    spread("G", 0, 256, (1,)); spread("S", 0, 256, (2, 3)); spread("G", 256, 512, (1, 2, 3)); le[0]()
    frac(LO, 0); d2(0); rl[1](); rh[1](); d2(1); le[1](); d2(2); frac(HI, 1); frac(HI, 0); d2(3)
    spread("G", 512, 768, (1, 2))

    slope(0, 256); far_v(0, 256); far_add(0, 256)
    le[3](); le[2](); slope(256, 512); far_v(256, 512); far_add(256, 512)
    halo_mm(); le[4]()
    for b in range(4):
        cl(b); dl(b)
    seam(); spread("S", 512, 768, (3,)); spread("G", 768, 1024, (1, 2))

    slope(512, 768); far_v(512, 768); far_add(512, 768)
    quant_w()
    for b in range(4):
        cr(b); dr(b)
    spread("S", 768, 1024, (3,))
    P = 888
    slope(768, P); far_v(768, P); far_add(768, P)
    quant_m(0, 512); products(0, 512, (4, 5))
    slope(P, 1024)
    for o in range(2):
        to_y(0, 512, (4, 5), "SSSS", (o,)); store("Y", TC * o + 128, TC * o + 384)
    quant_m(512, 768); products(512, 768, (6, 7))
    tap(P, 1024)
    for o in range(2):
        to_y(512, 768, (6, 7), "SSSS", (o,)); store("Y", TC * o, TC * o + 128)
    quant_m(768, 1024); products(768, 1024, (2, 3))
    for o in range(2):
        to_y(768, 1024, (2, 3), "VVVV", (o,)); store("YS"[o], TC * o + 384, TC * o + TC)
    g.wait_ge(T.sem.sent, sent)
    drain("Y")
